import numpy as np
import ml_dtypes


def mxq(x, axis, fmt="e4m3"):
    dtype, down = {"e4m3": (ml_dtypes.float8_e4m3fn, 7), "e5m2": (ml_dtypes.float8_e5m2, 14)}[fmt]
    v = np.moveaxis(np.asarray(x, np.float32).astype(ml_dtypes.bfloat16).astype(np.float64), axis, -1)
    blocks = v.reshape(v.shape[:-1] + (-1, 32))
    amax = np.abs(blocks).max(-1, keepdims=True)
    byte = np.maximum(np.where(amax > 0, np.frexp(amax)[1] - 1 + 127, 0) - down, 1)
    scale = np.exp2(byte - 127.0)
    codes = (blocks / scale).astype(np.float32).astype(dtype).astype(np.float64)
    return np.moveaxis((codes * scale).reshape(v.shape), -1, axis)


WIDE = False


def mx_kscale(k):
    if not WIDE:
        return np.ones(k)
    levels = np.array([18, -18])
    if k % 512:
        return np.exp2(np.random.permutation(np.resize(levels, k // 32))).repeat(32)
    a = np.empty((k // 512, 16))
    for p in range(k // 512):
        a[p, :8] = np.random.permutation(np.resize(levels, 8))
        for g in range(8):
            far = levels[np.abs(levels - a[p, g]) >= 10]
            a[p, g + 8] = far[np.random.randint(len(far))]
    return np.exp2(a.ravel()).repeat(32)


def f64(x):
    return np.asarray(x).astype(np.float64)


def striped(idx):
    return np.tile(np.asarray(idx).reshape(-1, 16).T, (8, 1)).astype(np.uint16)


def unstriped(offs):
    return offs[:16].T.reshape(-1).astype(np.int64)


V, K, E, D, DV = 1024, 2, 2048, 512, 512


def setup_inputs():
    n = np.random.standard_normal
    v = mx_kscale(DV)[:, None]
    coarse = lambda x: x.astype(np.float32).astype(ml_dtypes.bfloat16).astype(np.float64)
    return {
        "dyT": (coarse(n((DV, V))) * v).astype(np.float32),
        "hE": coarse(n((DV, E))).astype(np.float32),
        "wm": (n((DV, D)) / np.sqrt(DV) / v).astype(np.float32),
        "offs": striped(np.random.randint(0, V, E)),
        "offs2": striped(np.random.permutation(E)),
    }


def reference(dyT, hE, wm, offs, offs2):
    h = f64(hE)
    dz = f64(dyT)[:, unstriped(offs)] * 2.0 * np.maximum(h, 0.0)
    dm = mxq(f64(wm), 0, "e4m3").T @ mxq(dz, 0, "e5m2")
    return dm[:, unstriped(offs2)].reshape(D, V, K).sum(-1)

@@ -1,0 +1,235 @@
+from contextlib import ExitStack
+
+import concourse.mybir as mybir
+from concourse.masks import make_identity
+
+V, K, E, D, DV = 1024, 2, 2048, 512, 512
+FLOPS = 2 * DV * D * E
+
+F32 = mybir.dt.float32
+BF16 = mybir.dt.bfloat16
+U32 = mybir.dt.uint32
+U16 = mybir.dt.uint16
+U8 = mybir.dt.uint8
+E4M3 = mybir.dt.float8_e4m3fn_x4
+E5M2 = mybir.dt.float8_e5m2_x4
+ALU = mybir.AluOpType
+ACT = mybir.ActivationFunctionType
+
+P = 128
+PACK = 4
+CHUNK = 512
+CHUNKS = E // CHUNK
+PER_COL = 16
+PIECES = ((0, 512), (512, 1024), (1024, 1536), (1536, 1920), (1920, 2048))
+
+
+def tile_attend_gmp_kernel(tc, dyT, hE, wm, offs, offs2, out):
+    nc = tc.nc
+    with ExitStack() as ctx:
+        keep = ctx.enter_context(tc.tile_pool(name="keep", bufs=1))
+        ring = ctx.enter_context(tc.tile_pool(name="ring", bufs=3))
+        psum_mm = ctx.enter_context(tc.psum_pool(name="psum_mm", bufs=4))
+        psum_tr = ctx.enter_context(tc.psum_pool(name="psum_tr", bufs=2))
+
+        dst_list = keep.tile([P, E // PER_COL], U16, name="dst_list")
+        src_list = keep.tile([P, E // PER_COL], U16, name="src_list")
+        dy = [keep.tile([P, V], F32, name=f"dy{t}") for t in range(PACK)]
+        h = [keep.tile([P, E], F32, name=f"h{t}") for t in range(PACK)]
+        dz = {a: keep.tile([P, PACK, b - a], F32, name=f"dz{a}") for a, b in PIECES}
+        dz_b = keep.tile([P, E, PACK], BF16, name="dz_b", align_bytes=64)
+        dz_codes = keep.tile([P, E], U32, name="dz_codes", align_bytes=64)
+        dz_scales = keep.tile([P, E], U8, name="dz_scales", align_bytes=64)
+        w_raw = keep.tile([P, PACK, D], F32, name="w_raw")
+        w_b = keep.tile([P, D, PACK], BF16, name="w_b", align_bytes=64)
+        w_codes = keep.tile([P, D], U32, name="w_codes", align_bytes=64)
+        w_scales = keep.tile([P, D], U8, name="w_scales", align_bytes=64)
+        dm = [keep.tile([P, E], F32, name=f"dm{i}") for i in range(D // P)]
+        ident0 = keep.tile([P, P], F32, name="ident0")
+        ident = keep.tile([P, P], F32, name="ident")
+
+        dy_rows = dyT.rearrange("(p t) v -> p t v", t=PACK)
+        h_rows = hE.rearrange("(p t) e -> p t e", t=PACK)
+
+        S, V_ = "scalar", "vector"
+
+        def load_list(k):
+            nc.sync.dma_start((dst_list, src_list)[k][:], (offs, offs2)[k])
+
+        def load_h(t, a, b):
+            nc.sync.dma_start(out=h[t][:, a:b], in_=h_rows[:, t, a:b])
+
+        def load_dy(t):
+            nc.sync.dma_start(out=dy[t][:], in_=dy_rows[:, t, :])
+
+        def load_w():
+            nc.sync.dma_start(out=w_raw[:], in_=wm.rearrange("(p t) d -> p t d", t=PACK))
+
+        def identity():
+            make_identity(nc, ident0[:])
+            nc.scalar.activation(ident[:], ident0[:], ACT.Relu)
+
+        def relu(e, t, a, b):
+            if e == S:
+                nc.scalar.activation(h[t][:, a:b], h[t][:, a:b], ACT.Relu, scale=2.0)
+            else:
+                nc.vector.tensor_scalar(h[t][:, a:b], h[t][:, a:b], 2.0, 0.0, ALU.mult, ALU.max)
+
+        def piece(a):
+            first = max(x for x in dz if x <= a)
+            return dz[first], first
+
+        def gather_dz(t, a, b):
+            tile, first = piece(a)
+            nc.vector.tensor_tensor(
+                tile[:, t, a - first : b - first],
+                dy[t][:].indirect(dst_list[:, a // PER_COL : b // PER_COL]),
+                h[t][:, a:b],
+                ALU.mult,
+            )
+
+        def interleave(e, dst, src):
+            copy = nc.scalar.copy if e == S else nc.vector.tensor_copy
+            copy(dst.rearrange("p (c i) t -> p c t i", i=4), src.rearrange("p t (c i) -> p c t i", i=4))
+
+        def cast_dz(e, a, b):
+            tile, first = piece(a)
+            interleave(e, dz_b[:, a:b, :], tile[:, :, a - first : b - first])
+
+        def cast_w(e, a, b):
+            interleave(e, w_b[:, a:b, :], w_raw[:, :, a:b])
+
+        def quantize(codes, scales, src, fmt, a, b):
+            nc.vector.quantize_mx(
+                out=codes[:, a:b].bitcast(fmt),
+                scales=scales[:, a:b],
+                in_=src[:, a:b, :].rearrange("p e t -> p (e t)"),
+            )
+
+        def quant_dz(a, b):
+            quantize(dz_codes, dz_scales, dz_b, E5M2, a, b)
+
+        def quant_w(a, b):
+            quantize(w_codes, w_scales, w_b, E4M3, a, b)
+
+        def product(i, c, e=S):
+            acc = psum_mm.tile([P, CHUNK], F32, name="acc")
+            nc.tensor.matmul_mx(
+                out=acc[:],
+                lhsT=w_codes[:, i * P : (i + 1) * P].bitcast(E4M3),
+                lhsT_scale=w_scales[:, i * P : (i + 1) * P],
+                rhs=dz_codes[:, c * CHUNK : (c + 1) * CHUNK].bitcast(E5M2),
+                rhs_scale=dz_scales[:, c * CHUNK : (c + 1) * CHUNK],
+                start=True,
+                stop=True,
+            )
+            copy = nc.scalar.copy if e == S else nc.vector.tensor_copy
+            copy(dm[i][:, c * CHUNK : (c + 1) * CHUNK], acc[:])
+
+        def gather_dm(i, a, b):
+            g = ring.tile([P, 1024], F32, name="g", bufs=8)
+            nc.vector.tensor_copy(g[:, : b - a], dm[i][:].indirect(src_list[:, a // PER_COL : b // PER_COL]))
+            return g
+
+        def store(i, a, b, res):
+            nc.sync.dma_start(out=out[i * P : (i + 1) * P, a // K : b // K], in_=res[:, : (b - a) // K])
+
+        def sum_tensor(i, a, b, g):
+            blocks = (b - a) // (K * P)
+            turned = psum_tr.tile([P, 4, P], F32, name="turned")
+            for x in range(blocks):
+                for j in range(K):
+                    nc.tensor.matmul(
+                        turned[:, x, :],
+                        g[:, K * P * x + j : K * P * (x + 1) : K],
+                        ident[:],
+                        start=(j == 0),
+                        stop=(j == K - 1),
+                        is_transpose=True,
+                    )
+            sums = ring.tile([P, 4, P], F32, name="sums")
+            nc.scalar.copy(sums[:, :blocks, :], turned[:, :blocks, :])
+            back = psum_tr.tile([P, 4, P], F32, name="back")
+            for x in range(blocks):
+                nc.tensor.transpose(back[:, x, :], sums[:, x, :], ident[:])
+            res = ring.tile([P, 512], F32, name="res", bufs=8)
+            nc.scalar.copy(res[:, : blocks * P], back[:, :blocks, :].rearrange("p x d -> p (x d)"))
+            store(i, a, b, res)
+
+        def sum_plain(e, i, a, b, g):
+            eng = nc.vector if e == V_ else nc.gpsimd
+            res = ring.tile([P, 512], F32, name="res", bufs=8)
+            eng.tensor_tensor(res[:, : (b - a) // K], g[:, 0 : b - a : K], g[:, 1 : b - a : K], ALU.add)
+            store(i, a, b, res)
+
+
+        load_list(0)
+        load_h(0, 0, 512)
+        load_dy(0)
+        load_h(0, 512, 1024)
+        for t in range(1, PACK):
+            load_h(t, 0, 512)
+            load_dy(t)
+            load_h(t, 512, 1024)
+        for t in range(PACK):
+            load_h(t, 1024, 2048)
+        load_w()
+        load_list(1)
+        identity()
+        for t in range(PACK):
+            for c in (0, 1):
+                relu(S, t, 512*c, 512*c+512)
+                gather_dz(t, 512*c, 512*c+512)
+        for t in range(PACK):
+            relu(S, t, 1024, 1536)
+            gather_dz(t, 1024, 1536)
+        cast_dz(S, 0, 256)
+        cast_dz(S, 256, 512)
+        for t in range(PACK):
+            relu(S, t, 1536, 2048)
+        cast_dz(S, 512, 1024)
+        cast_w(S, 0, 128)
+        for t in range(2):
+            gather_dz(t, 1536, 1920)
+        quant_dz(0, 512)
+        for t in range(2, 4):
+            gather_dz(t, 1536, 1920)
+        cast_dz(S, 1024, 1536)
+        for t in range(2):
+            gather_dz(t, 1920, 2048)
+        quant_dz(512, 1024)
+        quant_w(0, 128)
+        for t in range(2, 4):
+            gather_dz(t, 1920, 2048)
+        cast_dz(V_, 1536, 1792)
+        cast_dz(S, 1792, 1920)
+        quant_dz(1024, 1536)
+        cast_dz(V_, 1920, 2048)
+        product(0, 0)
+        product(0, 1)
+        product(0, 2)
+        quant_dz(1536, 1792)
+        quant_dz(1792, 2048)
+        product(0, 3)
+        cast_w(V_, 128, 512)
+        quant_w(128, 256)
+        quant_w(256, 512)
+        for i in range(1, 4):
+            for c in range(CHUNKS):
+                product(i, c)
+
+        for i in range(3):
+            g0 = gather_dm(i, 0, 1024)
+            g1 = gather_dm(i, 1024, 2048)
+            sum_tensor(i, 0, 1024, g0)
+            sum_tensor(i, 1024, 2048, g1)
+        ga = gather_dm(3, 0, 512)
+        gb = gather_dm(3, 512, 1024)
+        sum_tensor(3, 0, 512, ga)
+        gc = gather_dm(3, 1024, 1536)
+        sum_tensor(3, 512, 1024, gb)
+        gd = gather_dm(3, 1536, 1792)
+        sum_plain(V_, 3, 1024, 1536, gc)
+        ge = gather_dm(3, 1792, 2048)
+        sum_plain(V_, 3, 1536, 1792, gd)
+        sum_plain(V_, 3, 1792, 2048, ge)

@@ -21,6 +21,7 @@ PACK = 4
 CHUNK = 512
 CHUNKS = E // CHUNK
 PER_COL = 16
+LATE = 1792
 PIECES = ((0, 512), (512, 1024), (1024, 1536), (1536, 1920), (1920, 2048))
 
 
@@ -37,11 +38,12 @@ def tile_attend_gmp_kernel(tc, dyT, hE, wm, offs, offs2, out):
         dy = [keep.tile([P, V], F32, name=f"dy{t}") for t in range(PACK)]
         h = [keep.tile([P, E], F32, name=f"h{t}") for t in range(PACK)]
         dz = {a: keep.tile([P, PACK, b - a], F32, name=f"dz{a}") for a, b in PIECES}
-        dz_b = keep.tile([P, E, PACK], BF16, name="dz_b", align_bytes=64)
+        dz_b = keep.tile([P, LATE, PACK], BF16, name="dz_b", align_bytes=64)
+        dz_late = keep.tile([P, E - LATE, PACK], BF16, name="dz_late", tag="late", align_bytes=64)
         dz_codes = keep.tile([P, E], U32, name="dz_codes", align_bytes=64)
         dz_scales = keep.tile([P, E], U8, name="dz_scales", align_bytes=64)
         w_raw = keep.tile([P, PACK, D], F32, name="w_raw")
-        w_b = keep.tile([P, D, PACK], BF16, name="w_b", align_bytes=64)
+        w_b = keep.tile([P, P, PACK], BF16, name="w_b", align_bytes=64)
         w_codes = keep.tile([P, D], U32, name="w_codes", align_bytes=64)
         w_scales = keep.tile([P, D], U8, name="w_scales", align_bytes=64)
         dm = [keep.tile([P, E], F32, name=f"dm{i}") for i in range(D // P)]
@@ -92,25 +94,37 @@ def tile_attend_gmp_kernel(tc, dyT, hE, wm, offs, offs2, out):
             copy = nc.scalar.copy if e == S else nc.vector.tensor_copy
             copy(dst.rearrange("p (c i) t -> p c t i", i=4), src.rearrange("p t (c i) -> p c t i", i=4))
 
+        def dz_bf16(a, b):
+            return dz_b[:, a:b, :] if a < LATE else dz_late[:, a - LATE : b - LATE, :]
+
+        w_late = []
+
+        def w_bf16(a, b):
+            if a < P:
+                return w_b[:, a:b, :]
+            if not w_late:
+                w_late.append(keep.tile([P, D - P, PACK], BF16, name="w_late", tag="late", align_bytes=64))
+            return w_late[0][:, a - P : b - P, :]
+
         def cast_dz(e, a, b):
             tile, first = piece(a)
-            interleave(e, dz_b[:, a:b, :], tile[:, :, a - first : b - first])
+            interleave(e, dz_bf16(a, b), tile[:, :, a - first : b - first])
 
         def cast_w(e, a, b):
-            interleave(e, w_b[:, a:b, :], w_raw[:, :, a:b])
+            interleave(e, w_bf16(a, b), w_raw[:, :, a:b])
 
         def quantize(codes, scales, src, fmt, a, b):
             nc.vector.quantize_mx(
                 out=codes[:, a:b].bitcast(fmt),
                 scales=scales[:, a:b],
-                in_=src[:, a:b, :].rearrange("p e t -> p (e t)"),
+                in_=src.rearrange("p e t -> p (e t)"),
             )
 
         def quant_dz(a, b):
-            quantize(dz_codes, dz_scales, dz_b, E5M2, a, b)
+            quantize(dz_codes, dz_scales, dz_bf16(a, b), E5M2, a, b)
 
         def quant_w(a, b):
-            quantize(w_codes, w_scales, w_b, E4M3, a, b)
+            quantize(w_codes, w_scales, w_bf16(a, b), E4M3, a, b)
 
         def product(i, c, e=S):
             acc = psum_mm.tile([P, CHUNK], F32, name="acc")
@@ -175,7 +189,6 @@ def tile_attend_gmp_kernel(tc, dyT, hE, wm, offs, offs2, out):
             load_h(t, 1024, 2048)
         load_w()
         load_list(1)
-        identity()
         for t in range(PACK):
             for c in (0, 1):
                 relu(S, t, 512*c, 512*c+512)
@@ -221,15 +234,13 @@ def tile_attend_gmp_kernel(tc, dyT, hE, wm, offs, offs2, out):
         for i in range(3):
             g0 = gather_dm(i, 0, 1024)
             g1 = gather_dm(i, 1024, 2048)
-            sum_tensor(i, 0, 1024, g0)
-            sum_tensor(i, 1024, 2048, g1)
-        ga = gather_dm(3, 0, 512)
-        gb = gather_dm(3, 512, 1024)
-        sum_tensor(3, 0, 512, ga)
+            sum_plain("gpsimd", i, 0, 1024, g0)
+            sum_plain("gpsimd", i, 1024, 2048, g1)
+        ga = gather_dm(3, 0, 1024)
         gc = gather_dm(3, 1024, 1536)
-        sum_tensor(3, 512, 1024, gb)
+        sum_plain("gpsimd", 3, 0, 1024, ga)
         gd = gather_dm(3, 1536, 1792)
-        sum_plain(V_, 3, 1024, 1536, gc)
+        sum_plain("gpsimd", 3, 1024, 1536, gc)
         ge = gather_dm(3, 1792, 2048)
         sum_plain(V_, 3, 1536, 1792, gd)
         sum_plain(V_, 3, 1792, 2048, ge)

@@ -22,7 +22,7 @@ CHUNK = 512
 CHUNKS = E // CHUNK
 PER_COL = 16
 LATE = 1792
-PIECES = ((0, 512), (512, 1024), (1024, 1536), (1536, 1920), (1920, 2048))
+PIECES = ((0, 512), (512, 1024), (1024, 1536), (1536, 1792), (1792, 2048))
 
 
 def tile_attend_gmp_kernel(tc, dyT, hE, wm, offs, offs2, out):
@@ -42,13 +42,14 @@ def tile_attend_gmp_kernel(tc, dyT, hE, wm, offs, offs2, out):
         dz_late = keep.tile([P, E - LATE, PACK], BF16, name="dz_late", tag="late", align_bytes=64)
         dz_codes = keep.tile([P, E], U32, name="dz_codes", align_bytes=64)
         dz_scales = keep.tile([P, E], U8, name="dz_scales", align_bytes=64)
-        w_raw = keep.tile([P, PACK, D], F32, name="w_raw")
+        w_first = keep.tile([P, PACK, P], F32, name="w_first")
+        w_rest = keep.tile([P, PACK, D - P], F32, name="w_rest")
+        h_first = dy_first = None
         w_b = keep.tile([P, P, PACK], BF16, name="w_b", align_bytes=64)
         w_codes = keep.tile([P, D], U32, name="w_codes", align_bytes=64)
         w_scales = keep.tile([P, D], U8, name="w_scales", align_bytes=64)
         dm = [keep.tile([P, E], F32, name=f"dm{i}") for i in range(D // P)]
-        ident0 = keep.tile([P, P], F32, name="ident0")
-        ident = keep.tile([P, P], F32, name="ident")
+        ident0 = ident = None
 
         dy_rows = dyT.rearrange("(p t) v -> p t v", t=PACK)
         h_rows = hE.rearrange("(p t) e -> p t e", t=PACK)
@@ -64,8 +65,28 @@ def tile_attend_gmp_kernel(tc, dyT, hE, wm, offs, offs2, out):
         def load_dy(t):
             nc.sync.dma_start(out=dy[t][:], in_=dy_rows[:, t, :])
 
-        def load_w():
-            nc.sync.dma_start(out=w_raw[:], in_=wm.rearrange("(p t) d -> p t d", t=PACK))
+        def load_w(a, b):
+            nc.sync.dma_start(out=w_part(a)[:], in_=wm.rearrange("(p t) d -> p t d", t=PACK)[:, :, a:b])
+
+        def w_part(a):
+            return w_first if a < P else w_rest
+
+        def load_h4(a, b):
+            nc.sync.dma_start(out=h_first[:], in_=h_rows[:, :, a:b])
+
+        def relu4(a, b):
+            nc.scalar.activation(h_first[:], h_first[:], ACT.Relu, scale=2.0)
+
+        def gather_dy(t, a, b):
+            nc.vector.tensor_copy(dy_first[:, t, :], dy[t][:].indirect(dst_list[:, a // PER_COL : b // PER_COL]))
+
+        def mul_dz(a, b):
+            nc.vector.tensor_tensor(
+                dz_b[:, a:b, :].rearrange("p (c i) t -> p c t i", i=2),
+                dy_first[:].rearrange("p t (c i) -> p c t i", i=2),
+                h_first[:].rearrange("p t (c i) -> p c t i", i=2),
+                ALU.mult,
+            )
 
         def identity():
             make_identity(nc, ident0[:])
@@ -92,7 +113,7 @@ def tile_attend_gmp_kernel(tc, dyT, hE, wm, offs, offs2, out):
 
         def interleave(e, dst, src):
             copy = nc.scalar.copy if e == S else nc.vector.tensor_copy
-            copy(dst.rearrange("p (c i) t -> p c t i", i=4), src.rearrange("p t (c i) -> p c t i", i=4))
+            copy(dst.rearrange("p (c i) t -> p c t i", i=2), src.rearrange("p t (c i) -> p c t i", i=2))
 
         def dz_bf16(a, b):
             return dz_b[:, a:b, :] if a < LATE else dz_late[:, a - LATE : b - LATE, :]
@@ -111,7 +132,7 @@ def tile_attend_gmp_kernel(tc, dyT, hE, wm, offs, offs2, out):
             interleave(e, dz_bf16(a, b), tile[:, :, a - first : b - first])
 
         def cast_w(e, a, b):
-            interleave(e, w_bf16(a, b), w_raw[:, :, a:b])
+            interleave(e, w_bf16(a, b), w_part(a)[:])
 
         def quantize(codes, scales, src, fmt, a, b):
             nc.vector.quantize_mx(
@@ -181,40 +202,73 @@ def tile_attend_gmp_kernel(tc, dyT, hE, wm, offs, offs2, out):
         load_h(0, 0, 512)
         load_dy(0)
         load_h(0, 512, 1024)
-        for t in range(1, PACK):
-            load_h(t, 0, 512)
-            load_dy(t)
-            load_h(t, 512, 1024)
-        for t in range(PACK):
-            load_h(t, 1024, 2048)
-        load_w()
+        load_h(1, 0, 512)
+        load_dy(1)
+        load_h(1, 512, 1024)
+        load_h(2, 0, 512)
+        load_dy(2)
+        load_h(2, 512, 1024)
+        load_h(3, 0, 512)
+        load_dy(3)
+        load_h(3, 512, 1024)
+        load_h(0, 1024, 1536)
+        load_h(1, 1024, 1536)
+        load_h(2, 1024, 1536)
+        load_h(3, 1024, 1536)
+        load_w(0, 128)
+        load_h(0, 1536, 2048)
+        load_h(1, 1536, 2048)
+        load_h(2, 1536, 2048)
+        load_h(3, 1536, 2048)
+        load_w(128, 512)
         load_list(1)
-        for t in range(PACK):
-            for c in (0, 1):
-                relu(S, t, 512*c, 512*c+512)
-                gather_dz(t, 512*c, 512*c+512)
-        for t in range(PACK):
-            relu(S, t, 1024, 1536)
-            gather_dz(t, 1024, 1536)
+        relu(S, 0, 0, 512)
+        relu(S, 0, 512, 1024)
+        relu(S, 1, 0, 512)
+        relu(S, 1, 512, 1024)
+        relu(S, 2, 0, 512)
+        relu(S, 2, 512, 1024)
+        relu(S, 3, 0, 512)
+        relu(S, 3, 512, 1024)
+        relu(S, 0, 1024, 1536)
+        relu(S, 1, 1024, 1536)
+        relu(S, 2, 1024, 1536)
+        relu(S, 3, 1024, 1536)
+        relu(S, 0, 1536, 2048)
+        relu(S, 1, 1536, 2048)
+        relu(S, 2, 1536, 2048)
+        relu(S, 3, 1536, 2048)
+        gather_dz(0, 0, 512)
+        gather_dz(0, 512, 1024)
+        gather_dz(1, 0, 512)
+        gather_dz(1, 512, 1024)
+        gather_dz(2, 0, 512)
+        gather_dz(2, 512, 1024)
+        gather_dz(3, 0, 512)
+        gather_dz(3, 512, 1024)
         cast_dz(S, 0, 256)
         cast_dz(S, 256, 512)
-        for t in range(PACK):
-            relu(S, t, 1536, 2048)
-        cast_dz(S, 512, 1024)
+        cast_dz(S, 512, 768)
+        cast_dz(S, 768, 1024)
+        gather_dz(0, 1024, 1536)
+        gather_dz(1, 1024, 1536)
+        gather_dz(2, 1024, 1536)
+        gather_dz(3, 1024, 1536)
+        cast_dz(S, 1024, 1280)
+        cast_dz(S, 1280, 1536)
         cast_w(S, 0, 128)
-        for t in range(2):
-            gather_dz(t, 1536, 1920)
         quant_dz(0, 512)
-        for t in range(2, 4):
-            gather_dz(t, 1536, 1920)
-        cast_dz(S, 1024, 1536)
-        for t in range(2):
-            gather_dz(t, 1920, 2048)
+        gather_dz(0, 1536, 1792)
+        gather_dz(1, 1536, 1792)
+        gather_dz(2, 1536, 1792)
+        gather_dz(3, 1536, 1792)
+        cast_dz(S, 1536, 1792)
         quant_dz(512, 1024)
         quant_w(0, 128)
-        for t in range(2, 4):
-            gather_dz(t, 1920, 2048)
-        cast_dz(V_, 1536, 1792)
+        gather_dz(0, 1792, 2048)
+        gather_dz(1, 1792, 2048)
+        gather_dz(2, 1792, 2048)
+        gather_dz(3, 1792, 2048)
         cast_dz(S, 1792, 1920)
         quant_dz(1024, 1536)
         cast_dz(V_, 1920, 2048)

@@ -1,7 +1,6 @@
 from contextlib import ExitStack
 
 import concourse.mybir as mybir
-from concourse.masks import make_identity
 
 V, K, E, D, DV = 1024, 2, 2048, 512, 512
 FLOPS = 2 * DV * D * E
@@ -17,284 +16,163 @@ ALU = mybir.AluOpType
 ACT = mybir.ActivationFunctionType
 
 P = 128
-PACK = 4
+PLANES = 4
 CHUNK = 512
 CHUNKS = E // CHUNK
-PER_COL = 16
-LATE = 1792
-PIECES = ((0, 512), (512, 1024), (1024, 1536), (1536, 1792), (1792, 2048))
+HALF = CHUNK // 2
+BLOCKS = D // P
+PER_COLUMN = 16
+RUN = 2
+LOOKUP = E // 2
+LOOKUP_BUFS = 8
+PSUM_BUFS = 4
+
+LOADS = (
+    (0,), (0, 1), (1, 0), (1,), (1, 1), (0, 3), (2, 0), (2,), (2, 1), (3, 0), (3, 1), (3,),
+    (0, 2), (1, 2), (2, 2), (3, 2), (1, 3), (2, 3), (3, 3),
+)
 
 
 def tile_attend_gmp_kernel(tc, dyT, hE, wm, offs, offs2, out):
     nc = tc.nc
+    last_plane, last_chunk, last_block = PLANES - 1, CHUNKS - 1, BLOCKS - 1
     with ExitStack() as ctx:
         keep = ctx.enter_context(tc.tile_pool(name="keep", bufs=1))
-        ring = ctx.enter_context(tc.tile_pool(name="ring", bufs=3))
-        psum_mm = ctx.enter_context(tc.psum_pool(name="psum_mm", bufs=4))
-        psum_tr = ctx.enter_context(tc.psum_pool(name="psum_tr", bufs=2))
+        ring = ctx.enter_context(tc.tile_pool(name="ring", bufs=LOOKUP_BUFS))
+        psum = ctx.enter_context(tc.psum_pool(name="psum", bufs=PSUM_BUFS))
 
-        dst_list = keep.tile([P, E // PER_COL], U16, name="dst_list")
-        src_list = keep.tile([P, E // PER_COL], U16, name="src_list")
-        dy = [keep.tile([P, V], F32, name=f"dy{t}") for t in range(PACK)]
-        h = [keep.tile([P, E], F32, name=f"h{t}") for t in range(PACK)]
-        dz = {a: keep.tile([P, PACK, b - a], F32, name=f"dz{a}") for a, b in PIECES}
-        dz_b = keep.tile([P, LATE, PACK], BF16, name="dz_b", align_bytes=64)
-        dz_late = keep.tile([P, E - LATE, PACK], BF16, name="dz_late", tag="late", align_bytes=64)
-        dz_codes = keep.tile([P, E], U32, name="dz_codes", align_bytes=64)
-        dz_scales = keep.tile([P, E], U8, name="dz_scales", align_bytes=64)
-        w_first = keep.tile([P, PACK, P], F32, name="w_first")
-        w_rest = keep.tile([P, PACK, D - P], F32, name="w_rest")
-        h_first = dy_first = None
-        w_b = keep.tile([P, P, PACK], BF16, name="w_b", align_bytes=64)
+        dst_list = keep.tile([P, E // PER_COLUMN], U16, name="dst_list")
+        src_list = keep.tile([P, E // PER_COLUMN], U16, name="src_list")
+        dy = [keep.tile([P, V], F32, name=f"dy{t}") for t in range(PLANES)]
+        h = [keep.tile([P, E], F32, name=f"h{t}") for t in range(PLANES)]
+        dz = [keep.tile([P, PLANES, CHUNK], F32, name=f"dz{c}") for c in range(CHUNKS)]
+        dz_bf16 = [keep.tile([P, CHUNK, PLANES], BF16, name=f"dz_bf16_{c}", align_bytes=64) for c in range(CHUNKS)]
+        dz_codes = [keep.tile([P, CHUNK], U32, name=f"dz_codes{c}", align_bytes=64) for c in range(CHUNKS)]
+        dz_scales = [keep.tile([P, CHUNK], U8, name=f"dz_scales{c}", align_bytes=64) for c in range(CHUNKS)]
+        w_first = keep.tile([P, PLANES, P], F32, name="w_first")
+        w_rest = keep.tile([P, PLANES, D - P], F32, name="w_rest")
+        w_first_bf16 = keep.tile([P, P, PLANES], BF16, name="w_first_bf16", align_bytes=64)
         w_codes = keep.tile([P, D], U32, name="w_codes", align_bytes=64)
         w_scales = keep.tile([P, D], U8, name="w_scales", align_bytes=64)
-        dm = [keep.tile([P, E], F32, name=f"dm{i}") for i in range(D // P)]
-        ident0 = ident = None
+        dm = [keep.tile([P, E], F32, name=f"dm{i}") for i in range(BLOCKS)]
 
-        dy_rows = dyT.rearrange("(p t) v -> p t v", t=PACK)
-        h_rows = hE.rearrange("(p t) e -> p t e", t=PACK)
+        dy_planes = dyT.rearrange("(p t) v -> p t v", t=PLANES)
+        h_planes = hE.rearrange("(p t) e -> p t e", t=PLANES)
+        w_planes = wm.rearrange("(p t) d -> p t d", t=PLANES)
 
-        S, V_ = "scalar", "vector"
+        def edges(c):
+            return slice(c * CHUNK, (c + 1) * CHUNK)
 
-        def load_list(k):
-            nc.sync.dma_start((dst_list, src_list)[k][:], (offs, offs2)[k])
+        def entries(offsets, a, b):
+            return offsets[:, a // PER_COLUMN : b // PER_COLUMN]
 
-        def load_h(t, a, b):
-            nc.sync.dma_start(out=h[t][:, a:b], in_=h_rows[:, t, a:b])
+        def load_h(t, c):
+            nc.sync.dma_start(out=h[t][:, edges(c)], in_=h_planes[:, t, edges(c)])
 
-        def load_dy(t):
-            nc.sync.dma_start(out=dy[t][:], in_=dy_rows[:, t, :])
+        def relu(t, c):
+            nc.scalar.activation(h[t][:, edges(c)], h[t][:, edges(c)], ACT.Relu, scale=2.0)
 
-        def load_w(a, b):
-            nc.sync.dma_start(out=w_part(a)[:], in_=wm.rearrange("(p t) d -> p t d", t=PACK)[:, :, a:b])
+        def make_dz(t, c, a=0, b=CHUNK):
+            first = c * CHUNK
+            picked = dy[t][:].indirect(entries(dst_list, first + a, first + b))
+            nc.vector.tensor_tensor(dz[c][:, t, a:b], picked, h[t][:, first + a : first + b], ALU.mult)
 
-        def w_part(a):
-            return w_first if a < P else w_rest
+        def round_and_interleave(copy, dst, src):
+            copy(dst.rearrange("p (c i) t -> p c t i", i=RUN), src.rearrange("p t (c i) -> p c t i", i=RUN))
 
-        def load_h4(a, b):
-            nc.sync.dma_start(out=h_first[:], in_=h_rows[:, :, a:b])
+        def round_dz(copy, c, half):
+            cols = slice(half * HALF, (half + 1) * HALF)
+            round_and_interleave(copy, dz_bf16[c][:, cols, :], dz[c][:, :, cols])
 
-        def relu4(a, b):
-            nc.scalar.activation(h_first[:], h_first[:], ACT.Relu, scale=2.0)
+        def quantize(codes, scales, values, fmt):
+            nc.vector.quantize_mx(out=codes.bitcast(fmt), scales=scales, in_=values.rearrange("p c t -> p (c t)"))
 
-        def gather_dy(t, a, b):
-            nc.vector.tensor_copy(dy_first[:, t, :], dy[t][:].indirect(dst_list[:, a // PER_COL : b // PER_COL]))
+        def quantize_dz(c, a=0, b=CHUNK):
+            quantize(dz_codes[c][:, a:b], dz_scales[c][:, a:b], dz_bf16[c][:, a:b, :], E5M2)
 
-        def mul_dz(a, b):
-            nc.vector.tensor_tensor(
-                dz_b[:, a:b, :].rearrange("p (c i) t -> p c t i", i=2),
-                dy_first[:].rearrange("p t (c i) -> p c t i", i=2),
-                h_first[:].rearrange("p t (c i) -> p c t i", i=2),
-                ALU.mult,
-            )
-
-        def identity():
-            make_identity(nc, ident0[:])
-            nc.scalar.activation(ident[:], ident0[:], ACT.Relu)
-
-        def relu(e, t, a, b):
-            if e == S:
-                nc.scalar.activation(h[t][:, a:b], h[t][:, a:b], ACT.Relu, scale=2.0)
-            else:
-                nc.vector.tensor_scalar(h[t][:, a:b], h[t][:, a:b], 2.0, 0.0, ALU.mult, ALU.max)
-
-        def piece(a):
-            first = max(x for x in dz if x <= a)
-            return dz[first], first
-
-        def gather_dz(t, a, b):
-            tile, first = piece(a)
-            nc.vector.tensor_tensor(
-                tile[:, t, a - first : b - first],
-                dy[t][:].indirect(dst_list[:, a // PER_COL : b // PER_COL]),
-                h[t][:, a:b],
-                ALU.mult,
-            )
-
-        def interleave(e, dst, src):
-            copy = nc.scalar.copy if e == S else nc.vector.tensor_copy
-            copy(dst.rearrange("p (c i) t -> p c t i", i=2), src.rearrange("p t (c i) -> p c t i", i=2))
-
-        def dz_bf16(a, b):
-            return dz_b[:, a:b, :] if a < LATE else dz_late[:, a - LATE : b - LATE, :]
-
-        w_late = []
-
-        def w_bf16(a, b):
-            if a < P:
-                return w_b[:, a:b, :]
-            if not w_late:
-                w_late.append(keep.tile([P, D - P, PACK], BF16, name="w_late", tag="late", align_bytes=64))
-            return w_late[0][:, a - P : b - P, :]
-
-        def cast_dz(e, a, b):
-            tile, first = piece(a)
-            interleave(e, dz_bf16(a, b), tile[:, :, a - first : b - first])
-
-        def cast_w(e, a, b):
-            interleave(e, w_bf16(a, b), w_part(a)[:])
-
-        def quantize(codes, scales, src, fmt, a, b):
-            nc.vector.quantize_mx(
-                out=codes[:, a:b].bitcast(fmt),
-                scales=scales[:, a:b],
-                in_=src.rearrange("p e t -> p (e t)"),
-            )
-
-        def quant_dz(a, b):
-            quantize(dz_codes, dz_scales, dz_bf16(a, b), E5M2, a, b)
-
-        def quant_w(a, b):
-            quantize(w_codes, w_scales, w_bf16(a, b), E4M3, a, b)
-
-        def product(i, c, e=S):
-            acc = psum_mm.tile([P, CHUNK], F32, name="acc")
+        def make_dm(i, c):
+            features = slice(i * P, (i + 1) * P)
+            acc = psum.tile([P, CHUNK], F32, name="acc")
             nc.tensor.matmul_mx(
                 out=acc[:],
-                lhsT=w_codes[:, i * P : (i + 1) * P].bitcast(E4M3),
-                lhsT_scale=w_scales[:, i * P : (i + 1) * P],
-                rhs=dz_codes[:, c * CHUNK : (c + 1) * CHUNK].bitcast(E5M2),
-                rhs_scale=dz_scales[:, c * CHUNK : (c + 1) * CHUNK],
+                lhsT=w_codes[:, features].bitcast(E4M3),
+                lhsT_scale=w_scales[:, features],
+                rhs=dz_codes[c][:].bitcast(E5M2),
+                rhs_scale=dz_scales[c][:],
                 start=True,
                 stop=True,
             )
-            copy = nc.scalar.copy if e == S else nc.vector.tensor_copy
-            copy(dm[i][:, c * CHUNK : (c + 1) * CHUNK], acc[:])
+            nc.scalar.copy(dm[i][:, edges(c)], acc[:])
 
-        def gather_dm(i, a, b):
-            g = ring.tile([P, 1024], F32, name="g", bufs=8)
-            nc.vector.tensor_copy(g[:, : b - a], dm[i][:].indirect(src_list[:, a // PER_COL : b // PER_COL]))
-            return g
+        def look_up_dm(i, a, b):
+            picked = ring.tile([P, LOOKUP], F32, name="picked")
+            nc.vector.tensor_copy(picked[:, : b - a], dm[i][:].indirect(entries(src_list, a, b)))
+            return picked
 
-        def store(i, a, b, res):
-            nc.sync.dma_start(out=out[i * P : (i + 1) * P, a // K : b // K], in_=res[:, : (b - a) // K])
+        def add_and_store(engine, i, a, b, picked):
+            nodes = (b - a) // K
+            sums = ring.tile([P, LOOKUP // K], F32, name="sums")
+            engine.tensor_tensor(sums[:, :nodes], picked[:, 0 : b - a : K], picked[:, 1 : b - a : K], ALU.add)
+            nc.sync.dma_start(out=out[i * P : (i + 1) * P, a // K : b // K], in_=sums[:, :nodes])
 
-        def sum_tensor(i, a, b, g):
-            blocks = (b - a) // (K * P)
-            turned = psum_tr.tile([P, 4, P], F32, name="turned")
-            for x in range(blocks):
-                for j in range(K):
-                    nc.tensor.matmul(
-                        turned[:, x, :],
-                        g[:, K * P * x + j : K * P * (x + 1) : K],
-                        ident[:],
-                        start=(j == 0),
-                        stop=(j == K - 1),
-                        is_transpose=True,
-                    )
-            sums = ring.tile([P, 4, P], F32, name="sums")
-            nc.scalar.copy(sums[:, :blocks, :], turned[:, :blocks, :])
-            back = psum_tr.tile([P, 4, P], F32, name="back")
-            for x in range(blocks):
-                nc.tensor.transpose(back[:, x, :], sums[:, x, :], ident[:])
-            res = ring.tile([P, 512], F32, name="res", bufs=8)
-            nc.scalar.copy(res[:, : blocks * P], back[:, :blocks, :].rearrange("p x d -> p (x d)"))
-            store(i, a, b, res)
+        load_h(0, 0)
+        nc.sync.dma_start(dst_list[:], offs)
+        for load in LOADS:
+            if len(load) == 1:
+                nc.sync.dma_start(out=dy[load[0]][:], in_=dy_planes[:, load[0], :])
+            else:
+                load_h(*load)
+        nc.sync.dma_start(out=w_first[:], in_=w_planes[:, :, :P])
+        nc.sync.dma_start(out=w_rest[:], in_=w_planes[:, :, P:])
+        nc.sync.dma_start(src_list[:], offs2)
 
-        def sum_plain(e, i, a, b, g):
-            eng = nc.vector if e == V_ else nc.gpsimd
-            res = ring.tile([P, 512], F32, name="res", bufs=8)
-            eng.tensor_tensor(res[:, : (b - a) // K], g[:, 0 : b - a : K], g[:, 1 : b - a : K], ALU.add)
-            store(i, a, b, res)
+        pieces = [(t, c) for t in range(PLANES) for c in (0, 1)]
+        pieces += [(t, c) for c in range(2, CHUNKS) for t in range(PLANES)][:-1]
+        for t, c in pieces:
+            relu(t, c)
+        for t, c in pieces:
+            make_dz(t, c)
 
+        halves = [(c, half) for c in range(last_chunk) for half in (0, 1)]
+        for c, half in halves[:3]:
+            round_dz(nc.scalar.copy, c, half)
+        round_and_interleave(nc.scalar.copy, w_first_bf16[:], w_first[:])
+        relu(last_plane, last_chunk)
+        for c, half in halves[3:]:
+            round_dz(nc.scalar.copy, c, half)
+        quantize_dz(0)
+        quantize(w_codes[:, :P], w_scales[:, :P], w_first_bf16[:], E4M3)
+        make_dz(last_plane, last_chunk, 0, HALF)
+        make_dz(last_plane, last_chunk, HALF, CHUNK)
 
-        load_list(0)
-        load_h(0, 0, 512)
-        load_dy(0)
-        load_h(0, 512, 1024)
-        load_h(1, 0, 512)
-        load_dy(1)
-        load_h(1, 512, 1024)
-        load_h(2, 0, 512)
-        load_dy(2)
-        load_h(2, 512, 1024)
-        load_h(3, 0, 512)
-        load_dy(3)
-        load_h(3, 512, 1024)
-        load_h(0, 1024, 1536)
-        load_h(1, 1024, 1536)
-        load_h(2, 1024, 1536)
-        load_h(3, 1024, 1536)
-        load_w(0, 128)
-        load_h(0, 1536, 2048)
-        load_h(1, 1536, 2048)
-        load_h(2, 1536, 2048)
-        load_h(3, 1536, 2048)
-        load_w(128, 512)
-        load_list(1)
-        relu(S, 0, 0, 512)
-        relu(S, 0, 512, 1024)
-        relu(S, 1, 0, 512)
-        relu(S, 1, 512, 1024)
-        relu(S, 2, 0, 512)
-        relu(S, 2, 512, 1024)
-        relu(S, 3, 0, 512)
-        relu(S, 3, 512, 1024)
-        relu(S, 0, 1024, 1536)
-        relu(S, 1, 1024, 1536)
-        relu(S, 2, 1024, 1536)
-        relu(S, 3, 1024, 1536)
-        relu(S, 0, 1536, 2048)
-        relu(S, 1, 1536, 2048)
-        relu(S, 2, 1536, 2048)
-        relu(S, 3, 1536, 2048)
-        gather_dz(0, 0, 512)
-        gather_dz(0, 512, 1024)
-        gather_dz(1, 0, 512)
-        gather_dz(1, 512, 1024)
-        gather_dz(2, 0, 512)
-        gather_dz(2, 512, 1024)
-        gather_dz(3, 0, 512)
-        gather_dz(3, 512, 1024)
-        cast_dz(S, 0, 256)
-        cast_dz(S, 256, 512)
-        cast_dz(S, 512, 768)
-        cast_dz(S, 768, 1024)
-        gather_dz(0, 1024, 1536)
-        gather_dz(1, 1024, 1536)
-        gather_dz(2, 1024, 1536)
-        gather_dz(3, 1024, 1536)
-        cast_dz(S, 1024, 1280)
-        cast_dz(S, 1280, 1536)
-        cast_w(S, 0, 128)
-        quant_dz(0, 512)
-        gather_dz(0, 1536, 1792)
-        gather_dz(1, 1536, 1792)
-        gather_dz(2, 1536, 1792)
-        gather_dz(3, 1536, 1792)
-        cast_dz(S, 1536, 1792)
-        quant_dz(512, 1024)
-        quant_w(0, 128)
-        gather_dz(0, 1792, 2048)
-        gather_dz(1, 1792, 2048)
-        gather_dz(2, 1792, 2048)
-        gather_dz(3, 1792, 2048)
-        cast_dz(S, 1792, 1920)
-        quant_dz(1024, 1536)
-        cast_dz(V_, 1920, 2048)
-        product(0, 0)
-        product(0, 1)
-        product(0, 2)
-        quant_dz(1536, 1792)
-        quant_dz(1792, 2048)
-        product(0, 3)
-        cast_w(V_, 128, 512)
-        quant_w(128, 256)
-        quant_w(256, 512)
-        for i in range(1, 4):
+        round_dz(nc.scalar.copy, last_chunk, 1)
+        for c in range(1, last_chunk):
+            quantize_dz(c)
+        round_dz(nc.vector.tensor_copy, last_chunk, 0)
+        for c in range(last_chunk):
+            make_dm(0, c)
+        quantize_dz(last_chunk, HALF, CHUNK)
+        quantize_dz(last_chunk, 0, HALF)
+        make_dm(0, last_chunk)
+
+        w_rest_bf16 = keep.tile([P, D - P, PLANES], BF16, name=f"dz_bf16_{last_chunk}", align_bytes=64)
+        parts = ((P, 2 * P), (2 * P, D))
+        for a, b in parts:
+            round_and_interleave(nc.vector.tensor_copy, w_rest_bf16[:, a - P : b - P, :], w_rest[:, :, a - P : b - P])
+        for a, b in parts:
+            quantize(w_codes[:, a:b], w_scales[:, a:b], w_rest_bf16[:, a - P : b - P, :], E4M3)
+        for i in range(1, BLOCKS):
             for c in range(CHUNKS):
-                product(i, c)
+                make_dm(i, c)
 
-        for i in range(3):
-            g0 = gather_dm(i, 0, 1024)
-            g1 = gather_dm(i, 1024, 2048)
-            sum_plain("gpsimd", i, 0, 1024, g0)
-            sum_plain("gpsimd", i, 1024, 2048, g1)
-        ga = gather_dm(3, 0, 1024)
-        gc = gather_dm(3, 1024, 1536)
-        sum_plain("gpsimd", 3, 0, 1024, ga)
-        gd = gather_dm(3, 1536, 1792)
-        sum_plain("gpsimd", 3, 1024, 1536, gc)
-        ge = gather_dm(3, 1792, 2048)
-        sum_plain(V_, 3, 1536, 1792, gd)
-        sum_plain(V_, 3, 1792, 2048, ge)
+        for i in range(last_block):
+            spans = ((0, LOOKUP), (LOOKUP, E))
+            picked = [look_up_dm(i, a, b) for a, b in spans]
+            for (a, b), columns in zip(spans, picked):
+                add_and_store(nc.gpsimd, i, a, b, columns)
+
+        cuts = (0, E // 2, 3 * E // 4, 7 * E // 8, E)
+        spans = list(zip(cuts, cuts[1:]))
+        picked = [look_up_dm(last_block, a, b) for a, b in spans]
+        for engine, (a, b), columns in zip((nc.gpsimd, nc.gpsimd, nc.vector, nc.vector), spans, picked):
+            add_and_store(engine, last_block, a, b, columns)

@@ -19,18 +19,15 @@ P = 128
 PLANES = 4
 CHUNK = 512
 CHUNKS = E // CHUNK
-HALF = CHUNK // 2
+QUARTER = CHUNK // 4
 BLOCKS = D // P
 PER_COLUMN = 16
 RUN = 2
 LOOKUP = E // 2
 LOOKUP_BUFS = 8
 PSUM_BUFS = 4
-
-LOADS = (
-    (0,), (0, 1), (1, 0), (1,), (1, 1), (0, 3), (2, 0), (2,), (2, 1), (3, 0), (3, 1), (3,),
-    (0, 2), (1, 2), (2, 2), (3, 2), (1, 3), (2, 3), (3, 3),
-)
+SPARE = 32
+HALF = CHUNK // 2
 
 
 def tile_attend_gmp_kernel(tc, dyT, hE, wm, offs, offs2, out):
@@ -43,10 +40,12 @@ def tile_attend_gmp_kernel(tc, dyT, hE, wm, offs, offs2, out):
 
         dst_list = keep.tile([P, E // PER_COLUMN], U16, name="dst_list")
         src_list = keep.tile([P, E // PER_COLUMN], U16, name="src_list")
-        dy = [keep.tile([P, V], F32, name=f"dy{t}") for t in range(PLANES)]
+        dy = [keep.tile([P, V + SPARE], F32, name=f"dy{t}") for t in range(PLANES)]
         h = [keep.tile([P, E], F32, name=f"h{t}") for t in range(PLANES)]
-        dz = [keep.tile([P, PLANES, CHUNK], F32, name=f"dz{c}") for c in range(CHUNKS)]
-        dz_bf16 = [keep.tile([P, CHUNK, PLANES], BF16, name=f"dz_bf16_{c}", align_bytes=64) for c in range(CHUNKS)]
+        dz_early = keep.tile([P, PLANES, 2 * CHUNK], F32, name="dz_early")
+        dz_late = [keep.tile([P, PLANES, CHUNK], F32, name=f"dz{c}") for c in range(2, CHUNKS)]
+        dz_bf16 = {c: keep.tile([P, CHUNK, PLANES], BF16, name=f"dz_bf16_{c}", align_bytes=64) for c in range(1, CHUNKS)}
+        h_raw = keep.tile([P, 2, CHUNK], F32, name="dz_bf16_0", align_bytes=64)
         dz_codes = [keep.tile([P, CHUNK], U32, name=f"dz_codes{c}", align_bytes=64) for c in range(CHUNKS)]
         dz_scales = [keep.tile([P, CHUNK], U8, name=f"dz_scales{c}", align_bytes=64) for c in range(CHUNKS)]
         w_first = keep.tile([P, PLANES, P], F32, name="w_first")
@@ -60,29 +59,37 @@ def tile_attend_gmp_kernel(tc, dyT, hE, wm, offs, offs2, out):
         h_planes = hE.rearrange("(p t) e -> p t e", t=PLANES)
         w_planes = wm.rearrange("(p t) d -> p t d", t=PLANES)
 
-        def edges(c):
-            return slice(c * CHUNK, (c + 1) * CHUNK)
+        def edges(c, a=0, b=CHUNK):
+            return slice(c * CHUNK + a, c * CHUNK + b)
+
+        def dz_cols(c, a, b):
+            return dz_early[:, :, edges(c, a, b)] if c < 2 else dz_late[c - 2][:, :, a:b]
 
         def entries(offsets, a, b):
             return offsets[:, a // PER_COLUMN : b // PER_COLUMN]
 
-        def load_h(t, c):
-            nc.sync.dma_start(out=h[t][:, edges(c)], in_=h_planes[:, t, edges(c)])
+        def load_h(t, c, a=0, b=CHUNK):
+            nc.sync.dma_start(out=h[t][:, edges(c, a, b)], in_=h_planes[:, t, edges(c, a, b)])
 
-        def relu(t, c):
-            nc.scalar.activation(h[t][:, edges(c)], h[t][:, edges(c)], ACT.Relu, scale=2.0)
+        def load_dy(t):
+            nc.sync.dma_start(out=dy[t][:, :V], in_=dy_planes[:, t, :])
+
+        def relu(t, c, a=0, b=CHUNK):
+            nc.scalar.activation(h[t][:, edges(c, a, b)], h[t][:, edges(c, a, b)], ACT.Relu, scale=2.0)
+
+        def relu_on_vector(t, c, a=0, b=CHUNK):
+            nc.vector.tensor_scalar(h[t][:, edges(c, a, b)], h[t][:, edges(c, a, b)], 0.0, 2.0, ALU.max, ALU.mult)
 
         def make_dz(t, c, a=0, b=CHUNK):
             first = c * CHUNK
             picked = dy[t][:].indirect(entries(dst_list, first + a, first + b))
-            nc.vector.tensor_tensor(dz[c][:, t, a:b], picked, h[t][:, first + a : first + b], ALU.mult)
+            nc.vector.tensor_tensor(dz_cols(c, a, b)[:, t, :], picked, h[t][:, first + a : first + b], ALU.mult)
 
         def round_and_interleave(copy, dst, src):
             copy(dst.rearrange("p (c i) t -> p c t i", i=RUN), src.rearrange("p t (c i) -> p c t i", i=RUN))
 
-        def round_dz(copy, c, half):
-            cols = slice(half * HALF, (half + 1) * HALF)
-            round_and_interleave(copy, dz_bf16[c][:, cols, :], dz[c][:, :, cols])
+        def round_dz(copy, c, a, b):
+            round_and_interleave(copy, dz_bf16[c][:, a:b, :], dz_cols(c, a, b))
 
         def quantize(codes, scales, values, fmt):
             nc.vector.quantize_mx(out=codes.bitcast(fmt), scales=scales, in_=values.rearrange("p c t -> p (c t)"))
@@ -115,40 +122,58 @@ def tile_attend_gmp_kernel(tc, dyT, hE, wm, offs, offs2, out):
             engine.tensor_tensor(sums[:, :nodes], picked[:, 0 : b - a : K], picked[:, 1 : b - a : K], ALU.add)
             nc.sync.dma_start(out=out[i * P : (i + 1) * P, a // K : b // K], in_=sums[:, :nodes])
 
+        for t in range(PLANES):
+            nc.gpsimd.memset(dy[t][:, V:], 0.0)
         load_h(0, 0)
         nc.sync.dma_start(dst_list[:], offs)
-        for load in LOADS:
-            if len(load) == 1:
-                nc.sync.dma_start(out=dy[load[0]][:], in_=dy_planes[:, load[0], :])
-            else:
-                load_h(*load)
+        load_dy(0)
+        load_h(0, 1)
+        load_h(0, last_chunk)
+        for t in range(1, PLANES):
+            load_h(t, 0, 0, 2 * CHUNK)
+            load_dy(t)
+        for t in range(2):
+            nc.sync.dma_start(out=h_raw[:, t, :], in_=h_planes[:, t, edges(2)])
+        for t in range(2, PLANES):
+            load_h(t, 2)
+        for t in range(1, PLANES):
+            load_h(t, last_chunk)
         nc.sync.dma_start(out=w_first[:], in_=w_planes[:, :, :P])
         nc.sync.dma_start(out=w_rest[:], in_=w_planes[:, :, P:])
         nc.sync.dma_start(src_list[:], offs2)
 
-        pieces = [(t, c) for t in range(PLANES) for c in (0, 1)]
-        pieces += [(t, c) for c in range(2, CHUNKS) for t in range(PLANES)][:-1]
-        for t, c in pieces:
+        for c in (0, 1, last_chunk):
+            relu(0, c)
+        for t in range(1, PLANES):
+            relu(t, 0, 0, 2 * CHUNK)
+        for t in range(2):
+            nc.scalar.activation(h[t][:, edges(2)], h_raw[:, t, :], ACT.Relu, scale=2.0)
+        late = [(2, 2), (3, 2), (1, 3), (2, 3)]
+        for t, c in late:
             relu(t, c)
-        for t, c in pieces:
+        for c in (0, 1, last_chunk):
+            make_dz(0, c)
+        for t in (1, 2):
+            make_dz(t, 0, 0, 2 * CHUNK)
+        for t, c in [(3, 0), (3, 1), (0, 2), (1, 2)] + late:
             make_dz(t, c)
-
-        halves = [(c, half) for c in range(last_chunk) for half in (0, 1)]
-        for c, half in halves[:3]:
-            round_dz(nc.scalar.copy, c, half)
+        dz_bf16[0] = keep.tile([P, CHUNK, PLANES], BF16, name="dz_bf16_0", align_bytes=64)
+        halves = [(c, a, a + HALF) for c in range(last_chunk) for a in (0, HALF)]
+        for c, a, b in halves[:3]:
+            round_dz(nc.scalar.copy, c, a, b)
         round_and_interleave(nc.scalar.copy, w_first_bf16[:], w_first[:])
         relu(last_plane, last_chunk)
-        for c, half in halves[3:]:
-            round_dz(nc.scalar.copy, c, half)
+        for c, a, b in halves[3:]:
+            round_dz(nc.scalar.copy, c, a, b)
         quantize_dz(0)
         quantize(w_codes[:, :P], w_scales[:, :P], w_first_bf16[:], E4M3)
         make_dz(last_plane, last_chunk, 0, HALF)
         make_dz(last_plane, last_chunk, HALF, CHUNK)
 
-        round_dz(nc.scalar.copy, last_chunk, 1)
+        round_dz(nc.scalar.copy, last_chunk, HALF, CHUNK)
         for c in range(1, last_chunk):
             quantize_dz(c)
-        round_dz(nc.vector.tensor_copy, last_chunk, 0)
+        round_dz(nc.vector.tensor_copy, last_chunk, 0, HALF)
         for c in range(last_chunk):
             make_dm(0, c)
         quantize_dz(last_chunk, HALF, CHUNK)
@@ -171,8 +196,8 @@ def tile_attend_gmp_kernel(tc, dyT, hE, wm, offs, offs2, out):
             for (a, b), columns in zip(spans, picked):
                 add_and_store(nc.gpsimd, i, a, b, columns)
 
-        cuts = (0, E // 2, 3 * E // 4, 7 * E // 8, E)
+        cuts = (0, 3 * E // 8, 5 * E // 8, 6 * E // 8, 7 * E // 8, E)
         spans = list(zip(cuts, cuts[1:]))
         picked = [look_up_dm(last_block, a, b) for a, b in spans]
-        for engine, (a, b), columns in zip((nc.gpsimd, nc.gpsimd, nc.vector, nc.vector), spans, picked):
+        for engine, (a, b), columns in zip((nc.gpsimd, nc.gpsimd, nc.gpsimd, nc.vector, nc.vector), spans, picked):
             add_and_store(engine, last_block, a, b, columns)

@@ -27,6 +27,7 @@ LOOKUP = E // 2
 LOOKUP_BUFS = 8
 PSUM_BUFS = 4
 SPARE = 32
+PAD = 16
 HALF = CHUNK // 2
 
 
@@ -42,11 +43,11 @@ def tile_attend_gmp_kernel(tc, dyT, hE, wm, offs, offs2, out):
         src_list = keep.tile([P, E // PER_COLUMN], U16, name="src_list")
         dy = [keep.tile([P, V + SPARE], F32, name=f"dy{t}") for t in range(PLANES)]
         h = [keep.tile([P, E], F32, name=f"h{t}") for t in range(PLANES)]
-        dz_early = keep.tile([P, PLANES, 2 * CHUNK], F32, name="dz_early")
-        dz_late = [keep.tile([P, PLANES, CHUNK], F32, name=f"dz{c}") for c in range(2, CHUNKS)]
+        dz_early = keep.tile([P, PLANES, 2 * CHUNK + PAD], F32, name="dz_early")
+        dz_late = [keep.tile([P, PLANES, CHUNK + PAD], F32, name=f"dz{c}", align_bytes=64) for c in range(2, CHUNKS)]
         dz_bf16 = {c: keep.tile([P, CHUNK, PLANES], BF16, name=f"dz_bf16_{c}", align_bytes=64) for c in range(1, CHUNKS)}
         h_raw = keep.tile([P, 2, CHUNK], F32, name="dz_bf16_0", align_bytes=64)
-        dz_codes = [keep.tile([P, CHUNK], U32, name=f"dz_codes{c}", align_bytes=64) for c in range(CHUNKS)]
+        dz_codes = [keep.tile([P, CHUNK], U32, name=f"dz_codes{c}", align_bytes=64) for c in range(last_chunk)]
         dz_scales = [keep.tile([P, CHUNK], U8, name=f"dz_scales{c}", align_bytes=64) for c in range(CHUNKS)]
         w_first = keep.tile([P, PLANES, P], F32, name="w_first")
         w_rest = keep.tile([P, PLANES, D - P], F32, name="w_rest")
@@ -158,29 +159,30 @@ def tile_attend_gmp_kernel(tc, dyT, hE, wm, offs, offs2, out):
         for t, c in [(3, 0), (3, 1), (0, 2), (1, 2)] + late:
             make_dz(t, c)
         dz_bf16[0] = keep.tile([P, CHUNK, PLANES], BF16, name="dz_bf16_0", align_bytes=64)
-        halves = [(c, a, a + HALF) for c in range(last_chunk) for a in (0, HALF)]
-        for c, a, b in halves[:3]:
-            round_dz(nc.scalar.copy, c, a, b)
+        halves = ((0, HALF), (HALF, CHUNK))
+        for c in (0, 1):
+            for a, b in halves:
+                round_dz(nc.scalar.copy, c, a, b)
         round_and_interleave(nc.scalar.copy, w_first_bf16[:], w_first[:])
         relu(last_plane, last_chunk)
-        for c, a, b in halves[3:]:
-            round_dz(nc.scalar.copy, c, a, b)
-        quantize_dz(0)
+        for a, b in halves:
+            round_dz(nc.scalar.copy, 2, a, b)
+        for c in (0, 1):
+            quantize_dz(c)
         quantize(w_codes[:, :P], w_scales[:, :P], w_first_bf16[:], E4M3)
-        make_dz(last_plane, last_chunk, 0, HALF)
-        make_dz(last_plane, last_chunk, HALF, CHUNK)
+        for a, b in halves:
+            make_dz(last_plane, last_chunk, a, b)
 
         round_dz(nc.scalar.copy, last_chunk, HALF, CHUNK)
-        for c in range(1, last_chunk):
-            quantize_dz(c)
         round_dz(nc.vector.tensor_copy, last_chunk, 0, HALF)
-        for c in range(last_chunk):
+        quantize_dz(2)
+        dz_codes.append(keep.tile([P, CHUNK], U32, name="dz2", align_bytes=64))
+        for a, b in halves:
+            quantize_dz(last_chunk, a, b)
+        for c in range(CHUNKS):
             make_dm(0, c)
-        quantize_dz(last_chunk, HALF, CHUNK)
-        quantize_dz(last_chunk, 0, HALF)
-        make_dm(0, last_chunk)
 
-        w_rest_bf16 = keep.tile([P, D - P, PLANES], BF16, name=f"dz_bf16_{last_chunk}", align_bytes=64)
+        w_rest_bf16 = keep.tile([P, D - P, PLANES], BF16, name=f"dz{last_chunk}", align_bytes=64)
         parts = ((P, 2 * P), (2 * P, D))
         for a, b in parts:
             round_and_interleave(nc.vector.tensor_copy, w_rest_bf16[:, a - P : b - P, :], w_rest[:, :, a - P : b - P])

@@ -24,11 +24,12 @@ BLOCKS = D // P
 PER_COLUMN = 16
 RUN = 2
 LOOKUP = E // 2
-LOOKUP_BUFS = 8
+LOOKUP_BUFS = 5
 PSUM_BUFS = 4
 SPARE = 32
 PAD = 16
 HALF = CHUNK // 2
+VECTOR_ROUNDS = 160
 
 
 def tile_attend_gmp_kernel(tc, dyT, hE, wm, offs, offs2, out):
@@ -43,18 +44,23 @@ def tile_attend_gmp_kernel(tc, dyT, hE, wm, offs, offs2, out):
         src_list = keep.tile([P, E // PER_COLUMN], U16, name="src_list")
         dy = [keep.tile([P, V + SPARE], F32, name=f"dy{t}") for t in range(PLANES)]
         h = [keep.tile([P, E], F32, name=f"h{t}") for t in range(PLANES)]
-        dz_early = keep.tile([P, PLANES, 2 * CHUNK + PAD], F32, name="dz_early")
+        dz_early = keep.tile([P, PLANES, 2 * CHUNK + PAD], F32, name="dz_early", align_bytes=64)
         dz_late = [keep.tile([P, PLANES, CHUNK + PAD], F32, name=f"dz{c}", align_bytes=64) for c in range(2, CHUNKS)]
-        dz_bf16 = {c: keep.tile([P, CHUNK, PLANES], BF16, name=f"dz_bf16_{c}", align_bytes=64) for c in range(1, CHUNKS)}
+        dz_bf16 = {c: keep.tile([P, CHUNK, PLANES], BF16, name=f"dz_bf16_{c}", align_bytes=64) for c in (2,)}
         h_raw = keep.tile([P, 2, CHUNK], F32, name="dz_bf16_0", align_bytes=64)
-        dz_codes = [keep.tile([P, CHUNK], U32, name=f"dz_codes{c}", align_bytes=64) for c in range(last_chunk)]
-        dz_scales = [keep.tile([P, CHUNK], U8, name=f"dz_scales{c}", align_bytes=64) for c in range(CHUNKS)]
+        early_codes = keep.tile([P, 2 * CHUNK], U32, name="early_codes", align_bytes=64)
+        early_scales = keep.tile([P, 2 * CHUNK], U8, name="early_scales", align_bytes=64)
+        codes2 = keep.tile([P, CHUNK], U32, name="codes2", align_bytes=64)
+        late_scales = [keep.tile([P, CHUNK], U8, name=f"dz_scales{c}", align_bytes=64) for c in range(2, CHUNKS)]
+        dz_codes = [early_codes[:, :CHUNK], early_codes[:, CHUNK:], codes2[:]]
+        dz_scales = [early_scales[:, :CHUNK], early_scales[:, CHUNK:], late_scales[0][:], late_scales[1][:]]
         w_first = keep.tile([P, PLANES, P], F32, name="w_first")
         w_rest = keep.tile([P, PLANES, D - P], F32, name="w_rest")
         w_first_bf16 = keep.tile([P, P, PLANES], BF16, name="w_first_bf16", align_bytes=64)
         w_codes = keep.tile([P, D], U32, name="w_codes", align_bytes=64)
         w_scales = keep.tile([P, D], U8, name="w_scales", align_bytes=64)
-        dm = [keep.tile([P, E], F32, name=f"dm{i}") for i in range(BLOCKS)]
+        dm_all = keep.tile([P, BLOCKS * E], F32, name="dm_all")
+        dm_start = [(last_block - i) * E for i in range(BLOCKS)]
 
         dy_planes = dyT.rearrange("(p t) v -> p t v", t=PLANES)
         h_planes = hE.rearrange("(p t) e -> p t e", t=PLANES)
@@ -105,21 +111,23 @@ def tile_attend_gmp_kernel(tc, dyT, hE, wm, offs, offs2, out):
                 out=acc[:],
                 lhsT=w_codes[:, features].bitcast(E4M3),
                 lhsT_scale=w_scales[:, features],
-                rhs=dz_codes[c][:].bitcast(E5M2),
-                rhs_scale=dz_scales[c][:],
+                rhs=dz_codes[c].bitcast(E5M2),
+                rhs_scale=dz_scales[c],
                 start=True,
                 stop=True,
             )
-            nc.scalar.copy(dm[i][:, edges(c)], acc[:])
+            nc.scalar.copy(dm_all[:, dm_start[i] + c * CHUNK : dm_start[i] + (c + 1) * CHUNK], acc[:])
 
         def look_up_dm(i, a, b):
-            picked = ring.tile([P, LOOKUP], F32, name="picked")
-            nc.vector.tensor_copy(picked[:, : b - a], dm[i][:].indirect(entries(src_list, a, b)))
+            picked = ring.tile([P, E], F32, name="picked")
+            width = 2 * E if b - a == E else E
+            window = dm_all[:, dm_start[i] : dm_start[i] + width]
+            nc.vector.tensor_copy(picked[:, : b - a], window.indirect(entries(src_list, a, b)))
             return picked
 
         def add_and_store(engine, i, a, b, picked):
             nodes = (b - a) // K
-            sums = ring.tile([P, LOOKUP // K], F32, name="sums")
+            sums = ring.tile([P, E // K], F32, name="sums")
             engine.tensor_tensor(sums[:, :nodes], picked[:, 0 : b - a : K], picked[:, 1 : b - a : K], ALU.add)
             nc.sync.dma_start(out=out[i * P : (i + 1) * P, a // K : b // K], in_=sums[:, :nodes])
 
@@ -149,7 +157,7 @@ def tile_attend_gmp_kernel(tc, dyT, hE, wm, offs, offs2, out):
             relu(t, 0, 0, 2 * CHUNK)
         for t in range(2):
             nc.scalar.activation(h[t][:, edges(2)], h_raw[:, t, :], ACT.Relu, scale=2.0)
-        late = [(2, 2), (3, 2), (1, 3), (2, 3)]
+        late = [(2, 2), (3, 2), (1, 3), (2, 3), (3, 3)]
         for t, c in late:
             relu(t, c)
         for c in (0, 1, last_chunk):
@@ -158,48 +166,44 @@ def tile_attend_gmp_kernel(tc, dyT, hE, wm, offs, offs2, out):
             make_dz(t, 0, 0, 2 * CHUNK)
         for t, c in [(3, 0), (3, 1), (0, 2), (1, 2)] + late:
             make_dz(t, c)
-        dz_bf16[0] = keep.tile([P, CHUNK, PLANES], BF16, name="dz_bf16_0", align_bytes=64)
+        early_bf16 = keep.tile([P, 2 * CHUNK, PLANES], BF16, name="dz_bf16_0", align_bytes=64)
+        dz_bf16[0], dz_bf16[1] = early_bf16[:, :CHUNK, :], early_bf16[:, CHUNK:, :]
         halves = ((0, HALF), (HALF, CHUNK))
         for c in (0, 1):
             for a, b in halves:
                 round_dz(nc.scalar.copy, c, a, b)
         round_and_interleave(nc.scalar.copy, w_first_bf16[:], w_first[:])
-        relu(last_plane, last_chunk)
         for a, b in halves:
             round_dz(nc.scalar.copy, 2, a, b)
-        for c in (0, 1):
-            quantize_dz(c)
+        quantize(early_codes[:], early_scales[:], early_bf16[:], E5M2)
         quantize(w_codes[:, :P], w_scales[:, :P], w_first_bf16[:], E4M3)
-        for a, b in halves:
-            make_dz(last_plane, last_chunk, a, b)
 
-        round_dz(nc.scalar.copy, last_chunk, HALF, CHUNK)
-        round_dz(nc.vector.tensor_copy, last_chunk, 0, HALF)
+        dz_bf16[last_chunk] = keep.tile([P, CHUNK, PLANES], BF16, name="dz_early", align_bytes=64)
+        round_dz(nc.scalar.copy, last_chunk, VECTOR_ROUNDS, CHUNK)
+        round_dz(nc.vector.tensor_copy, last_chunk, 0, VECTOR_ROUNDS)
         quantize_dz(2)
-        dz_codes.append(keep.tile([P, CHUNK], U32, name="dz2", align_bytes=64))
-        for a, b in halves:
-            quantize_dz(last_chunk, a, b)
+        codes3 = keep.tile([P, CHUNK], U32, name="dz2", align_bytes=64)
+        dz_codes.append(codes3[:])
+        quantize_dz(last_chunk)
         for c in range(CHUNKS):
             make_dm(0, c)
 
         w_rest_bf16 = keep.tile([P, D - P, PLANES], BF16, name=f"dz{last_chunk}", align_bytes=64)
-        parts = ((P, 2 * P), (2 * P, D))
-        for a, b in parts:
-            round_and_interleave(nc.vector.tensor_copy, w_rest_bf16[:, a - P : b - P, :], w_rest[:, :, a - P : b - P])
-        for a, b in parts:
+        round_and_interleave(nc.vector.tensor_copy, w_rest_bf16[:], w_rest[:])
+        for a, b in ((P, 2 * P), (2 * P, D)):
             quantize(w_codes[:, a:b], w_scales[:, a:b], w_rest_bf16[:, a - P : b - P, :], E4M3)
         for i in range(1, BLOCKS):
             for c in range(CHUNKS):
                 make_dm(i, c)
 
         for i in range(last_block):
-            spans = ((0, LOOKUP), (LOOKUP, E))
+            spans = ((0, E),) if i > 0 else ((0, LOOKUP), (LOOKUP, E))
             picked = [look_up_dm(i, a, b) for a, b in spans]
             for (a, b), columns in zip(spans, picked):
                 add_and_store(nc.gpsimd, i, a, b, columns)
 
-        cuts = (0, 3 * E // 8, 5 * E // 8, 6 * E // 8, 7 * E // 8, E)
+        cuts = (0, E // 2, 3 * E // 4, 7 * E // 8, E)
         spans = list(zip(cuts, cuts[1:]))
         picked = [look_up_dm(last_block, a, b) for a, b in spans]
-        for engine, (a, b), columns in zip((nc.gpsimd, nc.gpsimd, nc.gpsimd, nc.vector, nc.vector), spans, picked):
+        for engine, (a, b), columns in zip((nc.gpsimd, nc.gpsimd, nc.vector, nc.vector), spans, picked):
             add_and_store(engine, last_block, a, b, columns)

@@ -19,109 +19,95 @@ P = 128
 PLANES = 4
 CHUNK = 512
 CHUNKS = E // CHUNK
-QUARTER = CHUNK // 4
+EARLY = 2 * CHUNK
 BLOCKS = D // P
 PER_COLUMN = 16
-RUN = 2
-LOOKUP = E // 2
-LOOKUP_BUFS = 5
-PSUM_BUFS = 4
+RUN = 4
 SPARE = 32
-PAD = 16
-HALF = CHUNK // 2
 VECTOR_ROUNDS = 160
+RING_BUFS = 5
+PSUM_BUFS = 4
 
 
 def tile_attend_gmp_kernel(tc, dyT, hE, wm, offs, offs2, out):
     nc = tc.nc
     last_plane, last_chunk, last_block = PLANES - 1, CHUNKS - 1, BLOCKS - 1
+    wide_planes = (1, 2)
     with ExitStack() as ctx:
         keep = ctx.enter_context(tc.tile_pool(name="keep", bufs=1))
-        ring = ctx.enter_context(tc.tile_pool(name="ring", bufs=LOOKUP_BUFS))
+        ring = ctx.enter_context(tc.tile_pool(name="ring", bufs=RING_BUFS))
         psum = ctx.enter_context(tc.psum_pool(name="psum", bufs=PSUM_BUFS))
+
+        def mx_tile(shape, dtype, name):
+            return keep.tile(shape, dtype, name=name, align_bytes=64)
 
         dst_list = keep.tile([P, E // PER_COLUMN], U16, name="dst_list")
         src_list = keep.tile([P, E // PER_COLUMN], U16, name="src_list")
-        dy = [keep.tile([P, V + SPARE], F32, name=f"dy{t}") for t in range(PLANES)]
+        dy = [keep.tile([P, V + SPARE * (t in wide_planes)], F32, name=f"dy{t}") for t in range(PLANES)]
         h = [keep.tile([P, E], F32, name=f"h{t}") for t in range(PLANES)]
-        dz_early = keep.tile([P, PLANES, 2 * CHUNK + PAD], F32, name="dz_early", align_bytes=64)
-        dz_late = [keep.tile([P, PLANES, CHUNK + PAD], F32, name=f"dz{c}", align_bytes=64) for c in range(2, CHUNKS)]
-        dz_bf16 = {c: keep.tile([P, CHUNK, PLANES], BF16, name=f"dz_bf16_{c}", align_bytes=64) for c in (2,)}
-        h_raw = keep.tile([P, 2, CHUNK], F32, name="dz_bf16_0", align_bytes=64)
-        early_codes = keep.tile([P, 2 * CHUNK], U32, name="early_codes", align_bytes=64)
-        early_scales = keep.tile([P, 2 * CHUNK], U8, name="early_scales", align_bytes=64)
-        codes2 = keep.tile([P, CHUNK], U32, name="codes2", align_bytes=64)
-        late_scales = [keep.tile([P, CHUNK], U8, name=f"dz_scales{c}", align_bytes=64) for c in range(2, CHUNKS)]
-        dz_codes = [early_codes[:, :CHUNK], early_codes[:, CHUNK:], codes2[:]]
-        dz_scales = [early_scales[:, :CHUNK], early_scales[:, CHUNK:], late_scales[0][:], late_scales[1][:]]
+        h_held = mx_tile([P, 2, CHUNK], F32, "buffer_a")
+        dz_early = mx_tile([P, PLANES, EARLY], F32, "buffer_b")
+        dz_late = {2: keep.tile([P, PLANES, CHUNK], F32, name="dz_chunk2"), 3: mx_tile([P, PLANES, CHUNK], F32, "buffer_c")}
         w_first = keep.tile([P, PLANES, P], F32, name="w_first")
         w_rest = keep.tile([P, PLANES, D - P], F32, name="w_rest")
-        w_first_bf16 = keep.tile([P, P, PLANES], BF16, name="w_first_bf16", align_bytes=64)
-        w_codes = keep.tile([P, D], U32, name="w_codes", align_bytes=64)
-        w_scales = keep.tile([P, D], U8, name="w_scales", align_bytes=64)
-        dm_all = keep.tile([P, BLOCKS * E], F32, name="dm_all")
+        w_codes = mx_tile([P, D], U32, "w_codes")
+        w_scales = mx_tile([P, D], U8, "w_scales")
+        dm = keep.tile([P, BLOCKS * E], F32, name="dm")
         dm_start = [(last_block - i) * E for i in range(BLOCKS)]
 
         dy_planes = dyT.rearrange("(p t) v -> p t v", t=PLANES)
         h_planes = hE.rearrange("(p t) e -> p t e", t=PLANES)
         w_planes = wm.rearrange("(p t) d -> p t d", t=PLANES)
 
-        def edges(c, a=0, b=CHUNK):
-            return slice(c * CHUNK + a, c * CHUNK + b)
-
-        def dz_cols(c, a, b):
-            return dz_early[:, :, edges(c, a, b)] if c < 2 else dz_late[c - 2][:, :, a:b]
+        def edges(c, count=CHUNK):
+            return slice(c * CHUNK, c * CHUNK + count)
 
         def entries(offsets, a, b):
             return offsets[:, a // PER_COLUMN : b // PER_COLUMN]
 
-        def load_h(t, c, a=0, b=CHUNK):
-            nc.sync.dma_start(out=h[t][:, edges(c, a, b)], in_=h_planes[:, t, edges(c, a, b)])
+        def load_h(t, c, count=CHUNK):
+            nc.sync.dma_start(out=h[t][:, edges(c, count)], in_=h_planes[:, t, edges(c, count)])
 
         def load_dy(t):
             nc.sync.dma_start(out=dy[t][:, :V], in_=dy_planes[:, t, :])
 
-        def relu(t, c, a=0, b=CHUNK):
-            nc.scalar.activation(h[t][:, edges(c, a, b)], h[t][:, edges(c, a, b)], ACT.Relu, scale=2.0)
+        def relu(dst, src):
+            nc.scalar.activation(dst, src, ACT.Relu, scale=2.0)
 
-        def relu_on_vector(t, c, a=0, b=CHUNK):
-            nc.vector.tensor_scalar(h[t][:, edges(c, a, b)], h[t][:, edges(c, a, b)], 0.0, 2.0, ALU.max, ALU.mult)
+        def relu_in_place(t, c, count=CHUNK):
+            relu(h[t][:, edges(c, count)], h[t][:, edges(c, count)])
 
-        def make_dz(t, c, a=0, b=CHUNK):
-            first = c * CHUNK
-            picked = dy[t][:].indirect(entries(dst_list, first + a, first + b))
-            nc.vector.tensor_tensor(dz_cols(c, a, b)[:, t, :], picked, h[t][:, first + a : first + b], ALU.mult)
+        def make_dz(t, c, count=CHUNK):
+            dst = dz_late[c][:, t, :] if c in dz_late else dz_early[:, t, edges(c, count)]
+            picked = dy[t][:].indirect(entries(dst_list, c * CHUNK, c * CHUNK + count))
+            nc.vector.tensor_tensor(dst, picked, h[t][:, edges(c, count)], ALU.mult)
 
         def round_and_interleave(copy, dst, src):
             copy(dst.rearrange("p (c i) t -> p c t i", i=RUN), src.rearrange("p t (c i) -> p c t i", i=RUN))
 
-        def round_dz(copy, c, a, b):
-            round_and_interleave(copy, dz_bf16[c][:, a:b, :], dz_cols(c, a, b))
-
         def quantize(codes, scales, values, fmt):
             nc.vector.quantize_mx(out=codes.bitcast(fmt), scales=scales, in_=values.rearrange("p c t -> p (c t)"))
 
-        def quantize_dz(c, a=0, b=CHUNK):
-            quantize(dz_codes[c][:, a:b], dz_scales[c][:, a:b], dz_bf16[c][:, a:b, :], E5M2)
-
         def make_dm(i, c):
             features = slice(i * P, (i + 1) * P)
+            codes, scales = dz_mx[c]
             acc = psum.tile([P, CHUNK], F32, name="acc")
             nc.tensor.matmul_mx(
                 out=acc[:],
                 lhsT=w_codes[:, features].bitcast(E4M3),
                 lhsT_scale=w_scales[:, features],
-                rhs=dz_codes[c].bitcast(E5M2),
-                rhs_scale=dz_scales[c],
+                rhs=codes.bitcast(E5M2),
+                rhs_scale=scales,
                 start=True,
                 stop=True,
             )
-            nc.scalar.copy(dm_all[:, dm_start[i] + c * CHUNK : dm_start[i] + (c + 1) * CHUNK], acc[:])
+            first = dm_start[i] + c * CHUNK
+            nc.scalar.copy(dm[:, first : first + CHUNK], acc[:])
 
         def look_up_dm(i, a, b):
-            picked = ring.tile([P, E], F32, name="picked")
             width = 2 * E if b - a == E else E
-            window = dm_all[:, dm_start[i] : dm_start[i] + width]
+            picked = ring.tile([P, E], F32, name="picked")
+            window = dm[:, dm_start[i] : dm_start[i] + width]
             nc.vector.tensor_copy(picked[:, : b - a], window.indirect(entries(src_list, a, b)))
             return picked
 
@@ -131,7 +117,7 @@ def tile_attend_gmp_kernel(tc, dyT, hE, wm, offs, offs2, out):
             engine.tensor_tensor(sums[:, :nodes], picked[:, 0 : b - a : K], picked[:, 1 : b - a : K], ALU.add)
             nc.sync.dma_start(out=out[i * P : (i + 1) * P, a // K : b // K], in_=sums[:, :nodes])
 
-        for t in range(PLANES):
+        for t in wide_planes:
             nc.gpsimd.memset(dy[t][:, V:], 0.0)
         load_h(0, 0)
         nc.sync.dma_start(dst_list[:], offs)
@@ -139,65 +125,71 @@ def tile_attend_gmp_kernel(tc, dyT, hE, wm, offs, offs2, out):
         load_h(0, 1)
         load_h(0, last_chunk)
         for t in range(1, PLANES):
-            load_h(t, 0, 0, 2 * CHUNK)
+            load_h(t, 0, EARLY)
             load_dy(t)
-        for t in range(2):
-            nc.sync.dma_start(out=h_raw[:, t, :], in_=h_planes[:, t, edges(2)])
-        for t in range(2, PLANES):
-            load_h(t, 2)
-        for t in range(1, PLANES):
-            load_h(t, last_chunk)
+        held = [(0, 2), (1, 2)]
+        late = [(2, 2), (3, 2), (1, 3), (2, 3), (3, 3)]
+        for k, (t, c) in enumerate(held):
+            nc.sync.dma_start(out=h_held[:, k, :], in_=h_planes[:, t, edges(c)])
+        for t, c in late:
+            load_h(t, c)
         nc.sync.dma_start(out=w_first[:], in_=w_planes[:, :, :P])
         nc.sync.dma_start(out=w_rest[:], in_=w_planes[:, :, P:])
         nc.sync.dma_start(src_list[:], offs2)
 
         for c in (0, 1, last_chunk):
-            relu(0, c)
+            relu_in_place(0, c)
         for t in range(1, PLANES):
-            relu(t, 0, 0, 2 * CHUNK)
-        for t in range(2):
-            nc.scalar.activation(h[t][:, edges(2)], h_raw[:, t, :], ACT.Relu, scale=2.0)
-        late = [(2, 2), (3, 2), (1, 3), (2, 3), (3, 3)]
+            relu_in_place(t, 0, EARLY)
+        for k, (t, c) in enumerate(held):
+            relu(h[t][:, edges(c)], h_held[:, k, :])
         for t, c in late:
-            relu(t, c)
+            relu_in_place(t, c)
         for c in (0, 1, last_chunk):
             make_dz(0, c)
-        for t in (1, 2):
-            make_dz(t, 0, 0, 2 * CHUNK)
-        for t, c in [(3, 0), (3, 1), (0, 2), (1, 2)] + late:
+        for t in wide_planes:
+            make_dz(t, 0, EARLY)
+        for t, c in [(last_plane, 0), (last_plane, 1)] + held + late:
             make_dz(t, c)
-        early_bf16 = keep.tile([P, 2 * CHUNK, PLANES], BF16, name="dz_bf16_0", align_bytes=64)
-        dz_bf16[0], dz_bf16[1] = early_bf16[:, :CHUNK, :], early_bf16[:, CHUNK:, :]
-        halves = ((0, HALF), (HALF, CHUNK))
+
+        early_bf16 = mx_tile([P, EARLY, PLANES], BF16, "buffer_a")
         for c in (0, 1):
-            for a, b in halves:
-                round_dz(nc.scalar.copy, c, a, b)
+            round_and_interleave(nc.scalar.copy, early_bf16[:, edges(c), :], dz_early[:, :, edges(c)])
+        w_first_bf16 = mx_tile([P, P, PLANES], BF16, "w_first_bf16")
         round_and_interleave(nc.scalar.copy, w_first_bf16[:], w_first[:])
-        for a, b in halves:
-            round_dz(nc.scalar.copy, 2, a, b)
+        chunk2_bf16 = mx_tile([P, CHUNK, PLANES], BF16, "chunk2_bf16")
+        round_and_interleave(nc.scalar.copy, chunk2_bf16[:], dz_late[2][:])
+        early_codes = mx_tile([P, EARLY], U32, "early_codes")
+        early_scales = mx_tile([P, EARLY], U8, "early_scales")
         quantize(early_codes[:], early_scales[:], early_bf16[:], E5M2)
         quantize(w_codes[:, :P], w_scales[:, :P], w_first_bf16[:], E4M3)
 
-        dz_bf16[last_chunk] = keep.tile([P, CHUNK, PLANES], BF16, name="dz_early", align_bytes=64)
-        round_dz(nc.scalar.copy, last_chunk, VECTOR_ROUNDS, CHUNK)
-        round_dz(nc.vector.tensor_copy, last_chunk, 0, VECTOR_ROUNDS)
-        quantize_dz(2)
-        codes3 = keep.tile([P, CHUNK], U32, name="dz2", align_bytes=64)
-        dz_codes.append(codes3[:])
-        quantize_dz(last_chunk)
+        chunk3_bf16 = mx_tile([P, CHUNK, PLANES], BF16, "buffer_b")
+        round_and_interleave(nc.scalar.copy, chunk3_bf16[:, VECTOR_ROUNDS:, :], dz_late[3][:, :, VECTOR_ROUNDS:])
+        round_and_interleave(nc.vector.tensor_copy, chunk3_bf16[:, :VECTOR_ROUNDS, :], dz_late[3][:, :, :VECTOR_ROUNDS])
+        chunk2_codes = mx_tile([P, CHUNK], U32, "chunk2_codes")
+        chunk2_scales = mx_tile([P, CHUNK], U8, "chunk2_scales")
+        quantize(chunk2_codes[:], chunk2_scales[:], chunk2_bf16[:], E5M2)
+        chunk3_codes = mx_tile([P, CHUNK], U32, "chunk3_codes")
+        chunk3_scales = mx_tile([P, CHUNK], U8, "chunk3_scales")
+        quantize(chunk3_codes[:], chunk3_scales[:], chunk3_bf16[:], E5M2)
+        dz_mx = [(early_codes[:, edges(c)], early_scales[:, edges(c)]) for c in (0, 1)]
+        dz_mx.extend([(chunk2_codes[:], chunk2_scales[:]), (chunk3_codes[:], chunk3_scales[:])])
         for c in range(CHUNKS):
             make_dm(0, c)
 
-        w_rest_bf16 = keep.tile([P, D - P, PLANES], BF16, name=f"dz{last_chunk}", align_bytes=64)
-        round_and_interleave(nc.vector.tensor_copy, w_rest_bf16[:], w_rest[:])
-        for a, b in ((P, 2 * P), (2 * P, D)):
-            quantize(w_codes[:, a:b], w_scales[:, a:b], w_rest_bf16[:, a - P : b - P, :], E4M3)
+        w_rest_bf16 = mx_tile([P, D - P, PLANES], BF16, "buffer_c")
+        parts = ((0, P), (P, D - P))
+        for a, b in parts:
+            round_and_interleave(nc.vector.tensor_copy, w_rest_bf16[:, a:b, :], w_rest[:, :, a:b])
+        for a, b in parts:
+            quantize(w_codes[:, P + a : P + b], w_scales[:, P + a : P + b], w_rest_bf16[:, a:b, :], E4M3)
         for i in range(1, BLOCKS):
             for c in range(CHUNKS):
                 make_dm(i, c)
 
         for i in range(last_block):
-            spans = ((0, E),) if i > 0 else ((0, LOOKUP), (LOOKUP, E))
+            spans = ((0, E // 2), (E // 2, E)) if i == 0 else ((0, E),)
             picked = [look_up_dm(i, a, b) for a, b in spans]
             for (a, b), columns in zip(spans, picked):
                 add_and_store(nc.gpsimd, i, a, b, columns)

@@ -7,6 +7,7 @@ FLOPS = 2 * DV * D * E
 
 F32 = mybir.dt.float32
 BF16 = mybir.dt.bfloat16
+I32 = mybir.dt.int32
 U32 = mybir.dt.uint32
 U16 = mybir.dt.uint16
 U8 = mybir.dt.uint8
@@ -19,183 +20,150 @@ P = 128
 PLANES = 4
 CHUNK = 512
 CHUNKS = E // CHUNK
-EARLY = 2 * CHUNK
 BLOCKS = D // P
 PER_COLUMN = 16
 RUN = 4
-SPARE = 32
-VECTOR_ROUNDS = 160
-RING_BUFS = 5
-PSUM_BUFS = 4
+WIDE = 2048
+BANKS = 8
+HALF = CHUNK // 2
 
 
 def tile_attend_gmp_kernel(tc, dyT, hE, wm, offs, offs2, out):
     nc = tc.nc
-    last_plane, last_chunk, last_block = PLANES - 1, CHUNKS - 1, BLOCKS - 1
-    wide_planes = (1, 2)
+    last_chunk, last_block = CHUNKS - 1, BLOCKS - 1
     with ExitStack() as ctx:
         keep = ctx.enter_context(tc.tile_pool(name="keep", bufs=1))
-        ring = ctx.enter_context(tc.tile_pool(name="ring", bufs=RING_BUFS))
-        psum = ctx.enter_context(tc.psum_pool(name="psum", bufs=PSUM_BUFS))
+        psum = ctx.enter_context(tc.psum_pool(name="psum", bufs=BANKS))
 
-        def mx_tile(shape, dtype, name):
+        def tile(shape, dtype, name):
             return keep.tile(shape, dtype, name=name, align_bytes=64)
 
         dst_list = keep.tile([P, E // PER_COLUMN], U16, name="dst_list")
         src_list = keep.tile([P, E // PER_COLUMN], U16, name="src_list")
-        dy = [keep.tile([P, V + SPARE * (t in wide_planes)], F32, name=f"dy{t}") for t in range(PLANES)]
-        h = [keep.tile([P, E], F32, name=f"h{t}") for t in range(PLANES)]
-        h_held = mx_tile([P, 2, CHUNK], F32, "buffer_a")
-        dz_early = mx_tile([P, PLANES, EARLY], F32, "buffer_b")
-        dz_late = {2: keep.tile([P, PLANES, CHUNK], F32, name="dz_chunk2"), 3: mx_tile([P, PLANES, CHUNK], F32, "buffer_c")}
-        w_first = keep.tile([P, PLANES, P], F32, name="w_first")
-        w_rest = keep.tile([P, PLANES, D - P], F32, name="w_rest")
-        w_codes = mx_tile([P, D], U32, "w_codes")
-        w_scales = mx_tile([P, D], U8, "w_scales")
-        dm = keep.tile([P, BLOCKS * E], F32, name="dm")
-        dm_start = [(last_block - i) * E for i in range(BLOCKS)]
+        dy = [tile([P, WIDE], F32, f"dy{t}") for t in range(PLANES)]
+        h = [tile([P, PLANES, CHUNK], F32, f"h{c}") for c in range(CHUNKS)]
+        g = [tile([P, PLANES, CHUNK], F32, f"g{c}") for c in range(CHUNKS)]
+        dz = [tile([P, CHUNK, PLANES], BF16, f"dz{c}") for c in range(CHUNKS)]
+        dz_codes = [tile([P, CHUNK], U32, f"dz_codes{c}") for c in range(CHUNKS)]
+        dz_scales = [tile([P, CHUNK], U8, f"dz_scales{c}") for c in range(CHUNKS)]
+        w = tile([P, PLANES, D], F32, "w")
+        w_codes = tile([P, D], U32, "w_codes")
+        w_scales = tile([P, D], U8, "w_scales")
+        dm = [tile([P, E], F32, f"dm{i}") for i in range(BLOCKS)]
 
         dy_planes = dyT.rearrange("(p t) v -> p t v", t=PLANES)
         h_planes = hE.rearrange("(p t) e -> p t e", t=PLANES)
         w_planes = wm.rearrange("(p t) d -> p t d", t=PLANES)
 
-        def edges(c, count=CHUNK):
-            return slice(c * CHUNK, c * CHUNK + count)
+        def edges(c):
+            return slice(c * CHUNK, (c + 1) * CHUNK)
 
         def entries(offsets, a, b):
             return offsets[:, a // PER_COLUMN : b // PER_COLUMN]
 
-        def load_h(t, c, count=CHUNK):
-            nc.sync.dma_start(out=h[t][:, edges(c, count)], in_=h_planes[:, t, edges(c, count)])
+        def load_h(c, a=0, b=CHUNK):
+            nc.sync.dma_start(out=h[c][:, :, a:b], in_=h_planes[:, :, c * CHUNK + a : c * CHUNK + b])
 
         def load_dy(t):
             nc.sync.dma_start(out=dy[t][:, :V], in_=dy_planes[:, t, :])
 
-        def relu(dst, src):
-            nc.scalar.activation(dst, src, ACT.Relu, scale=2.0)
+        def look_up_dy(engine, t, c):
+            picked = dy[t][:].indirect(entries(dst_list, c * CHUNK, (c + 1) * CHUNK))
+            dst = g[c][:, t, :]
+            if engine == "vector":
+                nc.vector.tensor_scalar(dst, picked, 2.0, 0.0, ALU.mult, ALU.add)
+            else:
+                nc.scalar.activation(dst, picked, ACT.Copy, scale=2.0)
 
-        def relu_in_place(t, c, count=CHUNK):
-            relu(h[t][:, edges(c, count)], h[t][:, edges(c, count)])
+        def make_dz(c, a, b):
+            nc.vector.scalar_tensor_tensor(
+                dz[c][:, a:b, :],
+                h[c][:, :, a:b].rearrange("p t e -> p e t"),
+                0.0,
+                g[c][:, :, a:b].rearrange("p t e -> p e t"),
+                ALU.max,
+                ALU.mult,
+            )
 
-        def make_dz(t, c, count=CHUNK):
-            dst = dz_late[c][:, t, :] if c in dz_late else dz_early[:, t, edges(c, count)]
-            picked = dy[t][:].indirect(entries(dst_list, c * CHUNK, c * CHUNK + count))
-            nc.vector.tensor_tensor(dst, picked, h[t][:, edges(c, count)], ALU.mult)
-
-        def round_and_interleave(copy, dst, src):
-            copy(dst.rearrange("p (c i) t -> p c t i", i=RUN), src.rearrange("p t (c i) -> p c t i", i=RUN))
+        def quantize_w(name, a, b):
+            w_bf16 = tile([P, b - a, PLANES], BF16, name)
+            nc.vector.tensor_copy(
+                w_bf16[:].rearrange("p (c i) t -> p c t i", i=RUN), w[:, :, a:b].rearrange("p t (c i) -> p c t i", i=RUN)
+            )
+            quantize(w_codes[:, a:b], w_scales[:, a:b], w_bf16[:], E4M3)
 
         def quantize(codes, scales, values, fmt):
             nc.vector.quantize_mx(out=codes.bitcast(fmt), scales=scales, in_=values.rearrange("p c t -> p (c t)"))
 
-        def make_dm(i, c):
+        def make_dm(copy, i, c):
             features = slice(i * P, (i + 1) * P)
-            codes, scales = dz_mx[c]
             acc = psum.tile([P, CHUNK], F32, name="acc")
             nc.tensor.matmul_mx(
                 out=acc[:],
                 lhsT=w_codes[:, features].bitcast(E4M3),
                 lhsT_scale=w_scales[:, features],
-                rhs=codes.bitcast(E5M2),
-                rhs_scale=scales,
+                rhs=dz_codes[c][:].bitcast(E5M2),
+                rhs_scale=dz_scales[c][:],
                 start=True,
                 stop=True,
             )
-            first = dm_start[i] + c * CHUNK
-            nc.scalar.copy(dm[:, first : first + CHUNK], acc[:])
+            copy(dm[i][:, edges(c)], acc[:])
 
-        def look_up_dm(i, a, b):
-            width = 2 * E if b - a == E else E
-            picked = ring.tile([P, E], F32, name="picked")
-            window = dm[:, dm_start[i] : dm_start[i] + width]
-            nc.vector.tensor_copy(picked[:, : b - a], window.indirect(entries(src_list, a, b)))
+        def look_up_dm(engine, i, a, b, name):
+            picked = tile([P, b - a], F32, name)
+            window = dm[i][:].indirect(entries(src_list, a, b))
+            if engine == "vector":
+                nc.vector.tensor_copy(picked[:], window)
+            else:
+                nc.scalar.activation(picked[:], window, ACT.Copy)
             return picked
 
-        def add_and_store(engine, i, a, b, picked):
+        def add_and_store(engine, i, a, b, picked, name):
             nodes = (b - a) // K
-            sums = ring.tile([P, E // K], F32, name="sums")
-            engine.tensor_tensor(sums[:, :nodes], picked[:, 0 : b - a : K], picked[:, 1 : b - a : K], ALU.add)
-            nc.sync.dma_start(out=out[i * P : (i + 1) * P, a // K : b // K], in_=sums[:, :nodes])
+            sums = tile([P, nodes], F32, name)
+            engine.tensor_tensor(sums[:], picked[:, 0 : b - a : K], picked[:, 1 : b - a : K], ALU.add)
+            nc.sync.dma_start(out=out[i * P : (i + 1) * P, a // K : b // K], in_=sums[:])
 
-        for t in wide_planes:
+        for t in range(PLANES):
             nc.gpsimd.memset(dy[t][:, V:], 0.0)
-        load_h(0, 0)
-        nc.sync.dma_start(dst_list[:], offs)
         load_dy(0)
-        load_h(0, 1)
-        load_h(0, last_chunk)
+        nc.sync.dma_start(dst_list[:], offs)
         for t in range(1, PLANES):
-            load_h(t, 0, EARLY)
             load_dy(t)
-        held = [(0, 2), (1, 2)]
-        late = [(2, 2), (3, 2), (1, 3), (2, 3), (3, 3)]
-        for k, (t, c) in enumerate(held):
-            nc.sync.dma_start(out=h_held[:, k, :], in_=h_planes[:, t, edges(c)])
-        for t, c in late:
-            load_h(t, c)
-        nc.sync.dma_start(out=w_first[:], in_=w_planes[:, :, :P])
-        nc.sync.dma_start(out=w_rest[:], in_=w_planes[:, :, P:])
+        load_h(0, 0, HALF)
+        load_h(0, HALF, CHUNK)
+        load_h(1)
+        nc.sync.dma_start(out=w[:], in_=w_planes)
+        load_h(2)
+        load_h(3)
         nc.sync.dma_start(src_list[:], offs2)
 
-        for c in (0, 1, last_chunk):
-            relu_in_place(0, c)
-        for t in range(1, PLANES):
-            relu_in_place(t, 0, EARLY)
-        for k, (t, c) in enumerate(held):
-            relu(h[t][:, edges(c)], h_held[:, k, :])
-        for t, c in late:
-            relu_in_place(t, c)
-        for c in (0, 1, last_chunk):
-            make_dz(0, c)
-        for t in wide_planes:
-            make_dz(t, 0, EARLY)
-        for t, c in [(last_plane, 0), (last_plane, 1)] + held + late:
-            make_dz(t, c)
-
-        early_bf16 = mx_tile([P, EARLY, PLANES], BF16, "buffer_a")
-        for c in (0, 1):
-            round_and_interleave(nc.scalar.copy, early_bf16[:, edges(c), :], dz_early[:, :, edges(c)])
-        w_first_bf16 = mx_tile([P, P, PLANES], BF16, "w_first_bf16")
-        round_and_interleave(nc.scalar.copy, w_first_bf16[:], w_first[:])
-        chunk2_bf16 = mx_tile([P, CHUNK, PLANES], BF16, "chunk2_bf16")
-        round_and_interleave(nc.scalar.copy, chunk2_bf16[:], dz_late[2][:])
-        early_codes = mx_tile([P, EARLY], U32, "early_codes")
-        early_scales = mx_tile([P, EARLY], U8, "early_scales")
-        quantize(early_codes[:], early_scales[:], early_bf16[:], E5M2)
-        quantize(w_codes[:, :P], w_scales[:, :P], w_first_bf16[:], E4M3)
-
-        chunk3_bf16 = mx_tile([P, CHUNK, PLANES], BF16, "buffer_b")
-        round_and_interleave(nc.scalar.copy, chunk3_bf16[:, VECTOR_ROUNDS:, :], dz_late[3][:, :, VECTOR_ROUNDS:])
-        round_and_interleave(nc.vector.tensor_copy, chunk3_bf16[:, :VECTOR_ROUNDS, :], dz_late[3][:, :, :VECTOR_ROUNDS])
-        chunk2_codes = mx_tile([P, CHUNK], U32, "chunk2_codes")
-        chunk2_scales = mx_tile([P, CHUNK], U8, "chunk2_scales")
-        quantize(chunk2_codes[:], chunk2_scales[:], chunk2_bf16[:], E5M2)
-        chunk3_codes = mx_tile([P, CHUNK], U32, "chunk3_codes")
-        chunk3_scales = mx_tile([P, CHUNK], U8, "chunk3_scales")
-        quantize(chunk3_codes[:], chunk3_scales[:], chunk3_bf16[:], E5M2)
-        dz_mx = [(early_codes[:, edges(c)], early_scales[:, edges(c)]) for c in (0, 1)]
-        dz_mx.extend([(chunk2_codes[:], chunk2_scales[:]), (chunk3_codes[:], chunk3_scales[:])])
         for c in range(CHUNKS):
-            make_dm(0, c)
+            for t in range(PLANES):
+                look_up_dy("vector" if c == 0 else "scalar", t, c)
+            for a in (0, HALF):
+                make_dz(c, a, a + HALF)
+            for a in (0, HALF):
+                quantize(dz_codes[c][:, a : a + HALF], dz_scales[c][:, a : a + HALF], dz[c][:, a : a + HALF, :], E5M2)
+            if c == 1:
+                quantize_w("w_early", 0, 2 * P)
+        for i in range(2):
+            for c in range(last_chunk):
+                make_dm(nc.scalar.copy, i, c)
+        for i in range(2):
+            make_dm(nc.scalar.copy, i, last_chunk)
+        quantize_w(f"dz{last_chunk}", 2 * P, D)
 
-        w_rest_bf16 = mx_tile([P, D - P, PLANES], BF16, "buffer_c")
-        parts = ((0, P), (P, D - P))
-        for a, b in parts:
-            round_and_interleave(nc.vector.tensor_copy, w_rest_bf16[:, a:b, :], w_rest[:, :, a:b])
-        for a, b in parts:
-            quantize(w_codes[:, P + a : P + b], w_scales[:, P + a : P + b], w_rest_bf16[:, a:b, :], E4M3)
-        for i in range(1, BLOCKS):
-            for c in range(CHUNKS):
-                make_dm(i, c)
-
-        for i in range(last_block):
-            spans = ((0, E // 2), (E // 2, E)) if i == 0 else ((0, E),)
-            picked = [look_up_dm(i, a, b) for a, b in spans]
-            for (a, b), columns in zip(spans, picked):
-                add_and_store(nc.gpsimd, i, a, b, columns)
-
-        cuts = (0, E // 2, 3 * E // 4, 7 * E // 8, E)
-        spans = list(zip(cuts, cuts[1:]))
-        picked = [look_up_dm(last_block, a, b) for a, b in spans]
-        for engine, (a, b), columns in zip((nc.gpsimd, nc.gpsimd, nc.vector, nc.vector), spans, picked):
-            add_and_store(engine, last_block, a, b, columns)
+        for i in range(BLOCKS):
+            if i == 0:
+                spans = [("vector", nc.gpsimd, 0, 512), ("scalar", nc.gpsimd, 512, 1248), ("vector", nc.gpsimd, 1248, E)]
+            elif i < last_block:
+                spans = [("scalar", nc.gpsimd, 0, 736), ("vector", nc.gpsimd, 736, E)]
+            else:
+                spans = [("vector", nc.gpsimd, 0, 800), ("scalar", nc.gpsimd, 800, 1280), ("vector", nc.vector, 1280, 1792), ("scalar", nc.vector, 1792, E)]
+            picked = [look_up_dm(e, i, a, b, f"picked{i}{a}") for e, adder, a, b in spans]
+            for (e, adder, a, b), columns in zip(spans, picked):
+                add_and_store(adder, i, a, b, columns, f"sums{i}{a}")
+            if i + 2 < BLOCKS:
+                for c in range(CHUNKS):
+                    make_dm(nc.scalar.copy, i + 2, c)

@@ -42,11 +42,12 @@ def tile_attend_gmp_kernel(tc, dyT, hE, wm, offs, offs2, out):
         src_list = keep.tile([P, E // PER_COLUMN], U16, name="src_list")
         dy = [tile([P, WIDE], F32, f"dy{t}") for t in range(PLANES)]
         h = [tile([P, PLANES, CHUNK], F32, f"h{c}") for c in range(CHUNKS)]
-        g = [tile([P, PLANES, CHUNK], F32, f"g{c}") for c in range(CHUNKS)]
-        dz = [tile([P, CHUNK, PLANES], BF16, f"dz{c}") for c in range(CHUNKS)]
+        g = {}
+        dz = {}
         dz_codes = [tile([P, CHUNK], U32, f"dz_codes{c}") for c in range(CHUNKS)]
         dz_scales = [tile([P, CHUNK], U8, f"dz_scales{c}") for c in range(CHUNKS)]
-        w = tile([P, PLANES, D], F32, "w")
+        w_early = tile([P, PLANES, D - P], F32, "w_early")
+        w_late = tile([P, PLANES, P], F32, "w_late")
         w_codes = tile([P, D], U32, "w_codes")
         w_scales = tile([P, D], U8, "w_scales")
         dm = [tile([P, E], F32, f"dm{i}") for i in range(BLOCKS)]
@@ -67,9 +68,9 @@ def tile_attend_gmp_kernel(tc, dyT, hE, wm, offs, offs2, out):
         def load_dy(t):
             nc.sync.dma_start(out=dy[t][:, :V], in_=dy_planes[:, t, :])
 
-        def look_up_dy(engine, t, c):
-            picked = dy[t][:].indirect(entries(dst_list, c * CHUNK, (c + 1) * CHUNK))
-            dst = g[c][:, t, :]
+        def look_up_dy(engine, t, c, a=0, b=CHUNK):
+            picked = dy[t][:].indirect(entries(dst_list, c * CHUNK + a, c * CHUNK + b))
+            dst = g[c][:, t, a:b]
             if engine == "vector":
                 nc.vector.tensor_scalar(dst, picked, 2.0, 0.0, ALU.mult, ALU.add)
             else:
@@ -85,12 +86,14 @@ def tile_attend_gmp_kernel(tc, dyT, hE, wm, offs, offs2, out):
                 ALU.mult,
             )
 
-        def quantize_w(name, a, b):
+        def quantize_w(name, w, a, b):
             w_bf16 = tile([P, b - a, PLANES], BF16, name)
             nc.vector.tensor_copy(
-                w_bf16[:].rearrange("p (c i) t -> p c t i", i=RUN), w[:, :, a:b].rearrange("p t (c i) -> p c t i", i=RUN)
+                w_bf16[:].rearrange("p (c i) t -> p c t i", i=RUN), w[:].rearrange("p t (c i) -> p c t i", i=RUN)
             )
-            quantize(w_codes[:, a:b], w_scales[:, a:b], w_bf16[:], E4M3)
+            for q in range(a, b, 2 * P):
+                r = min(q + 2 * P, b)
+                quantize(w_codes[:, q:r], w_scales[:, q:r], w_bf16[:, q - a : r - a, :], E4M3)
 
         def quantize(codes, scales, values, fmt):
             nc.vector.quantize_mx(out=codes.bitcast(fmt), scales=scales, in_=values.rearrange("p c t -> p (c t)"))
@@ -124,46 +127,56 @@ def tile_attend_gmp_kernel(tc, dyT, hE, wm, offs, offs2, out):
             engine.tensor_tensor(sums[:], picked[:, 0 : b - a : K], picked[:, 1 : b - a : K], ALU.add)
             nc.sync.dma_start(out=out[i * P : (i + 1) * P, a // K : b // K], in_=sums[:])
 
+        warm = tile([P, 2, 8], F32, "warm")
+        nc.gpsimd.memset(warm[:, 0, :], 0.0)
+        nc.scalar.activation(warm[:, 1, :], warm[:, 0, :], ACT.Copy)
         for t in range(PLANES):
-            nc.gpsimd.memset(dy[t][:, V:], 0.0)
+            (nc.vector if t < 2 else nc.gpsimd).memset(dy[t][:, V:], 0.0)
         load_dy(0)
         nc.sync.dma_start(dst_list[:], offs)
         for t in range(1, PLANES):
             load_dy(t)
         load_h(0, 0, HALF)
         load_h(0, HALF, CHUNK)
-        load_h(1)
-        nc.sync.dma_start(out=w[:], in_=w_planes)
-        load_h(2)
-        load_h(3)
+        nc.sync.dma_start(out=w_early[:], in_=w_planes[:, :, : D - P])
+        for c in range(1, CHUNKS):
+            load_h(c)
+        nc.sync.dma_start(out=w_late[:], in_=w_planes[:, :, D - P :])
         nc.sync.dma_start(src_list[:], offs2)
 
         for c in range(CHUNKS):
-            for t in range(PLANES):
-                look_up_dy("vector" if c == 0 else "scalar", t, c)
+            g[c] = tile([P, PLANES, CHUNK], F32, f"g{c % last_chunk}")
+            for a, b in ((0, CHUNK),) if c < last_chunk else ((0, HALF), (HALF, CHUNK)):
+                for t in range(PLANES):
+                    look_up_dy("vector" if c == 0 else "scalar", t, c, a, b)
+            dz[c] = tile([P, CHUNK, PLANES], BF16, f"dz{c}")
             for a in (0, HALF):
                 make_dz(c, a, a + HALF)
             for a in (0, HALF):
                 quantize(dz_codes[c][:, a : a + HALF], dz_scales[c][:, a : a + HALF], dz[c][:, a : a + HALF, :], E5M2)
-            if c == 1:
-                quantize_w("w_early", 0, 2 * P)
-        for i in range(2):
-            for c in range(last_chunk):
+            if c == 0:
+                quantize_w("dz1", w_early, 0, 3 * P)
+        for c in range(last_chunk):
+            for i in range(last_block):
                 make_dm(nc.scalar.copy, i, c)
-        for i in range(2):
-            make_dm(nc.scalar.copy, i, last_chunk)
-        quantize_w(f"dz{last_chunk}", 2 * P, D)
+        make_dm(nc.vector.tensor_copy, 0, last_chunk)
+        make_dm(nc.scalar.copy, 1, last_chunk)
+        make_dm(nc.scalar.copy, 2, last_chunk)
+        quantize_w(f"dz{last_chunk}", w_late, 3 * P, D)
 
+        picked = {}
         for i in range(BLOCKS):
+            spans = [("vector", 0, 576), ("vector", 576, 1152), ("scalar", 1152, E)]
             if i == 0:
-                spans = [("vector", nc.gpsimd, 0, 512), ("scalar", nc.gpsimd, 512, 1248), ("vector", nc.gpsimd, 1248, E)]
-            elif i < last_block:
-                spans = [("scalar", nc.gpsimd, 0, 736), ("vector", nc.gpsimd, 736, E)]
-            else:
-                spans = [("vector", nc.gpsimd, 0, 800), ("scalar", nc.gpsimd, 800, 1280), ("vector", nc.vector, 1280, 1792), ("scalar", nc.vector, 1792, E)]
-            picked = [look_up_dm(e, i, a, b, f"picked{i}{a}") for e, adder, a, b in spans]
-            for (e, adder, a, b), columns in zip(spans, picked):
-                add_and_store(adder, i, a, b, columns, f"sums{i}{a}")
-            if i + 2 < BLOCKS:
+                spans = [("vector", 0, 384), ("vector", 384, 1152), ("scalar", 1152, E)]
+            if i == last_block:
+                spans = [("vector", 0, 1088), ("scalar", 1088, 1792), ("scalar", 1792, E)]
+            for k, (e, a, b) in enumerate(spans):
+                picked[i, k] = (a, b, look_up_dm(e, i, a, b, f"picked{i}{a}"))
+            if i == 1:
                 for c in range(CHUNKS):
-                    make_dm(nc.scalar.copy, i + 2, c)
+                    make_dm(nc.scalar.copy, last_block, c)
+        order = [(0, 0), (0, 2), (0, 1), (1, 0), (1, 2), (1, 1), (2, 0), (2, 1), (2, 2), (3, 0), (3, 1), (3, 2)]
+        for n, (i, k) in enumerate(order):
+            a, b, columns = picked[i, k]
+            add_and_store(nc.gpsimd if n < len(order) - 3 else nc.vector, i, a, b, columns, f"sums{i}{a}")

@@ -46,8 +46,8 @@ def tile_attend_gmp_kernel(tc, dyT, hE, wm, offs, offs2, out):
         dz = {}
         dz_codes = [tile([P, CHUNK], U32, f"dz_codes{c}") for c in range(CHUNKS)]
         dz_scales = [tile([P, CHUNK], U8, f"dz_scales{c}") for c in range(CHUNKS)]
-        w_early = tile([P, PLANES, D - P], F32, "w_early")
-        w_late = tile([P, PLANES, P], F32, "w_late")
+        w_early = tile([P, PLANES, 2 * P], F32, "w_early")
+        w_late = tile([P, PLANES, 2 * P], F32, "g3")
         w_codes = tile([P, D], U32, "w_codes")
         w_scales = tile([P, D], U8, "w_scales")
         dm = [tile([P, E], F32, f"dm{i}") for i in range(BLOCKS)]
@@ -86,14 +86,10 @@ def tile_attend_gmp_kernel(tc, dyT, hE, wm, offs, offs2, out):
                 ALU.mult,
             )
 
-        def quantize_w(name, w, a, b):
-            w_bf16 = tile([P, b - a, PLANES], BF16, name)
-            nc.vector.tensor_copy(
-                w_bf16[:].rearrange("p (c i) t -> p c t i", i=RUN), w[:].rearrange("p t (c i) -> p c t i", i=RUN)
-            )
-            for q in range(a, b, 2 * P):
-                r = min(q + 2 * P, b)
-                quantize(w_codes[:, q:r], w_scales[:, q:r], w_bf16[:, q - a : r - a, :], E4M3)
+        def round_w(copy, name, w):
+            w_bf16 = tile([P, 2 * P, PLANES], BF16, name)
+            copy(w_bf16[:].rearrange("p (c i) t -> p c t i", i=RUN), w[:].rearrange("p t (c i) -> p c t i", i=RUN))
+            return w_bf16
 
         def quantize(codes, scales, values, fmt):
             nc.vector.quantize_mx(out=codes.bitcast(fmt), scales=scales, in_=values.rearrange("p c t -> p (c t)"))
@@ -138,45 +134,48 @@ def tile_attend_gmp_kernel(tc, dyT, hE, wm, offs, offs2, out):
             load_dy(t)
         load_h(0, 0, HALF)
         load_h(0, HALF, CHUNK)
-        nc.sync.dma_start(out=w_early[:], in_=w_planes[:, :, : D - P])
-        for c in range(1, CHUNKS):
-            load_h(c)
-        nc.sync.dma_start(out=w_late[:], in_=w_planes[:, :, D - P :])
+        nc.sync.dma_start(out=w_early[:], in_=w_planes[:, :, : 2 * P])
+        load_h(1)
+        nc.sync.dma_start(out=w_late[:], in_=w_planes[:, :, 2 * P :])
+        load_h(2)
+        load_h(3)
         nc.sync.dma_start(src_list[:], offs2)
 
         for c in range(CHUNKS):
-            g[c] = tile([P, PLANES, CHUNK], F32, f"g{c % last_chunk}")
+            g[c] = tile([P, PLANES, CHUNK], F32, f"g{c}")
             for a, b in ((0, CHUNK),) if c < last_chunk else ((0, HALF), (HALF, CHUNK)):
                 for t in range(PLANES):
                     look_up_dy("vector" if c == 0 else "scalar", t, c, a, b)
             dz[c] = tile([P, CHUNK, PLANES], BF16, f"dz{c}")
             for a in (0, HALF):
                 make_dz(c, a, a + HALF)
+            if c == 0:
+                w_bf16 = round_w(nc.vector.tensor_copy, "dz1", w_early)
             for a in (0, HALF):
                 quantize(dz_codes[c][:, a : a + HALF], dz_scales[c][:, a : a + HALF], dz[c][:, a : a + HALF, :], E5M2)
             if c == 0:
-                quantize_w("dz1", w_early, 0, 3 * P)
+                quantize(w_codes[:, : 2 * P], w_scales[:, : 2 * P], w_bf16[:], E4M3)
+            if c == 1:
+                w_bf16 = round_w(nc.scalar.copy, "w_late_bf16", w_late)
+                quantize(w_codes[:, 2 * P :], w_scales[:, 2 * P :], w_bf16[:], E4M3)
         for c in range(last_chunk):
-            for i in range(last_block):
+            for i in range(BLOCKS):
                 make_dm(nc.scalar.copy, i, c)
         make_dm(nc.vector.tensor_copy, 0, last_chunk)
         make_dm(nc.scalar.copy, 1, last_chunk)
-        make_dm(nc.scalar.copy, 2, last_chunk)
-        quantize_w(f"dz{last_chunk}", w_late, 3 * P, D)
 
         picked = {}
         for i in range(BLOCKS):
-            spans = [("vector", 0, 576), ("vector", 576, 1152), ("scalar", 1152, E)]
+            spans = [("vector", 0, 512), ("vector", 512, 1056), ("scalar", 1056, E)]
             if i == 0:
-                spans = [("vector", 0, 384), ("vector", 384, 1152), ("scalar", 1152, E)]
+                spans = [("vector", 0, 384), ("vector", 384, 1056), ("scalar", 1056, E)]
             if i == last_block:
-                spans = [("vector", 0, 1088), ("scalar", 1088, 1792), ("scalar", 1792, E)]
+                spans = [("vector", 0, 992), ("scalar", 992, 1792), ("scalar", 1792, E)]
             for k, (e, a, b) in enumerate(spans):
                 picked[i, k] = (a, b, look_up_dm(e, i, a, b, f"picked{i}{a}"))
-            if i == 1:
-                for c in range(CHUNKS):
-                    make_dm(nc.scalar.copy, last_block, c)
-        order = [(0, 0), (0, 2), (0, 1), (1, 0), (1, 2), (1, 1), (2, 0), (2, 1), (2, 2), (3, 0), (3, 1), (3, 2)]
+            if i + 2 < BLOCKS:
+                make_dm(nc.scalar.copy, i + 2, last_chunk)
+        order = [(0, 0), (0, 1), (0, 2), (1, 0), (1, 1), (1, 2), (2, 0), (2, 1), (2, 2), (3, 0), (3, 1), (3, 2)]
         for n, (i, k) in enumerate(order):
             a, b, columns = picked[i, k]
             add_and_store(nc.gpsimd if n < len(order) - 3 else nc.vector, i, a, b, columns, f"sums{i}{a}")

@@ -33,7 +33,7 @@ def tile_attend_gmp_kernel(tc, dyT, hE, wm, offs, offs2, out):
     last_chunk, last_block = CHUNKS - 1, BLOCKS - 1
     with ExitStack() as ctx:
         keep = ctx.enter_context(tc.tile_pool(name="keep", bufs=1))
-        psum = ctx.enter_context(tc.psum_pool(name="psum", bufs=BANKS))
+        psum = ctx.enter_context(tc.psum_pool(name="psum", bufs=1))
 
         def tile(shape, dtype, name):
             return keep.tile(shape, dtype, name=name, align_bytes=64)
@@ -46,11 +46,9 @@ def tile_attend_gmp_kernel(tc, dyT, hE, wm, offs, offs2, out):
         dz = {}
         dz_codes = [tile([P, CHUNK], U32, f"dz_codes{c}") for c in range(CHUNKS)]
         dz_scales = [tile([P, CHUNK], U8, f"dz_scales{c}") for c in range(CHUNKS)]
-        w_early = tile([P, PLANES, 2 * P], F32, "w_early")
-        w_late = tile([P, PLANES, 2 * P], F32, "g3")
-        w_codes = tile([P, D], U32, "w_codes")
-        w_scales = tile([P, D], U8, "w_scales")
-        dm = [tile([P, E], F32, f"dm{i}") for i in range(BLOCKS)]
+        w = tile([P, PLANES, D], F32, "w")
+        w_mx = {}
+        dm = {}
 
         dy_planes = dyT.rearrange("(p t) v -> p t v", t=PLANES)
         h_planes = hE.rearrange("(p t) e -> p t e", t=PLANES)
@@ -86,17 +84,23 @@ def tile_attend_gmp_kernel(tc, dyT, hE, wm, offs, offs2, out):
                 ALU.mult,
             )
 
-        def round_w(copy, name, w):
+        def round_w(copy, half, name):
             w_bf16 = tile([P, 2 * P, PLANES], BF16, name)
-            copy(w_bf16[:].rearrange("p (c i) t -> p c t i", i=RUN), w[:].rearrange("p t (c i) -> p c t i", i=RUN))
+            columns = w[:, :, half * 2 * P : (half + 1) * 2 * P]
+            copy(w_bf16[:].rearrange("p (c i) t -> p c t i", i=RUN), columns.rearrange("p t (c i) -> p c t i", i=RUN))
             return w_bf16
+
+        def quantize_w(half, w_bf16, name):
+            w_mx[half] = (tile([P, 2 * P], U32, name), tile([P, 2 * P], U8, f"w_scales{half}"))
+            quantize(w_mx[half][0][:], w_mx[half][1][:], w_bf16[:], E4M3)
 
         def quantize(codes, scales, values, fmt):
             nc.vector.quantize_mx(out=codes.bitcast(fmt), scales=scales, in_=values.rearrange("p c t -> p (c t)"))
 
-        def make_dm(copy, i, c):
-            features = slice(i * P, (i + 1) * P)
-            acc = psum.tile([P, CHUNK], F32, name="acc")
+        def make_dm(copy, i, c, bank):
+            w_codes, w_scales = w_mx[i // 2]
+            features = slice(i % 2 * P, (i % 2 + 1) * P)
+            acc = psum.tile([P, CHUNK], F32, name=f"bank{bank}")
             nc.tensor.matmul_mx(
                 out=acc[:],
                 lhsT=w_codes[:, features].bitcast(E4M3),
@@ -132,49 +136,55 @@ def tile_attend_gmp_kernel(tc, dyT, hE, wm, offs, offs2, out):
         nc.sync.dma_start(dst_list[:], offs)
         for t in range(1, PLANES):
             load_dy(t)
-        load_h(0, 0, HALF)
-        load_h(0, HALF, CHUNK)
-        nc.sync.dma_start(out=w_early[:], in_=w_planes[:, :, : 2 * P])
-        load_h(1)
-        nc.sync.dma_start(out=w_late[:], in_=w_planes[:, :, 2 * P :])
-        load_h(2)
-        load_h(3)
+        for c in (0, 1):
+            load_h(c, 0, HALF)
+            load_h(c, HALF, CHUNK)
+        nc.sync.dma_start(out=w[:], in_=w_planes)
+        for c in (2, 3):
+            load_h(c, 0, HALF)
+            load_h(c, HALF, CHUNK)
         nc.sync.dma_start(src_list[:], offs2)
 
         for c in range(CHUNKS):
-            g[c] = tile([P, PLANES, CHUNK], F32, f"g{c}")
+            g[c] = tile([P, PLANES, CHUNK], F32, f"g{c % last_chunk}")
             for a, b in ((0, CHUNK),) if c < last_chunk else ((0, HALF), (HALF, CHUNK)):
                 for t in range(PLANES):
                     look_up_dy("vector" if c == 0 else "scalar", t, c, a, b)
             dz[c] = tile([P, CHUNK, PLANES], BF16, f"dz{c}")
             for a in (0, HALF):
                 make_dz(c, a, a + HALF)
-            if c == 0:
-                w_bf16 = round_w(nc.vector.tensor_copy, "dz1", w_early)
+            if c == 1:
+                w_bf16 = round_w(nc.vector.tensor_copy, 0, "dz2")
             for a in (0, HALF):
                 quantize(dz_codes[c][:, a : a + HALF], dz_scales[c][:, a : a + HALF], dz[c][:, a : a + HALF, :], E5M2)
-            if c == 0:
-                quantize(w_codes[:, : 2 * P], w_scales[:, : 2 * P], w_bf16[:], E4M3)
             if c == 1:
-                w_bf16 = round_w(nc.scalar.copy, "w_late_bf16", w_late)
-                quantize(w_codes[:, 2 * P :], w_scales[:, 2 * P :], w_bf16[:], E4M3)
-        for c in range(last_chunk):
-            for i in range(BLOCKS):
-                make_dm(nc.scalar.copy, i, c)
-        make_dm(nc.vector.tensor_copy, 0, last_chunk)
-        make_dm(nc.scalar.copy, 1, last_chunk)
+                quantize_w(0, w_bf16, "w_codes0")
+            if c == 2:
+                quantize_w(1, round_w(nc.scalar.copy, 1, "w_bf16"), "h2")
+        for i in range(BLOCKS):
+            dm[i] = tile([P, E], F32, f"dm{i}" if i < last_block else f"dz{last_chunk}")
+        early = [(i, c) for c in range(last_chunk) for i in (0, 1)] + [(2, c) for c in range(last_chunk)]
+        for n, (i, c) in enumerate(early):
+            make_dm(nc.scalar.copy, i, c, n % BANKS)
+        make_dm(nc.vector.tensor_copy, last_block, 0, 1)
+        make_dm(nc.scalar.copy, last_block, 1, 2)
+        make_dm(nc.vector.tensor_copy, 0, last_chunk, 3)
+        make_dm(nc.scalar.copy, 1, last_chunk, 4)
 
         picked = {}
         for i in range(BLOCKS):
-            spans = [("vector", 0, 512), ("vector", 512, 1056), ("scalar", 1056, E)]
+            spans = [("vector", 0, 544), ("vector", 544, 1088), ("scalar", 1088, E)]
             if i == 0:
-                spans = [("vector", 0, 384), ("vector", 384, 1056), ("scalar", 1056, E)]
+                spans = [("vector", 0, 384), ("vector", 384, 1088), ("scalar", 1088, E)]
             if i == last_block:
-                spans = [("vector", 0, 992), ("scalar", 992, 1792), ("scalar", 1792, E)]
+                spans = [("vector", 0, 1024), ("scalar", 1024, 1792), ("scalar", 1792, E)]
             for k, (e, a, b) in enumerate(spans):
                 picked[i, k] = (a, b, look_up_dm(e, i, a, b, f"picked{i}{a}"))
-            if i + 2 < BLOCKS:
-                make_dm(nc.scalar.copy, i + 2, last_chunk)
+            if i == 0:
+                make_dm(nc.scalar.copy, 2, last_chunk, 5)
+            if i == 1:
+                make_dm(nc.scalar.copy, last_block, 2, 3)
+                make_dm(nc.scalar.copy, last_block, last_chunk, 6)
         order = [(0, 0), (0, 1), (0, 2), (1, 0), (1, 1), (1, 2), (2, 0), (2, 1), (2, 2), (3, 0), (3, 1), (3, 2)]
         for n, (i, k) in enumerate(order):
             a, b, columns = picked[i, k]

@@ -41,9 +41,10 @@ def tile_attend_gmp_kernel(tc, dyT, hE, wm, offs, offs2, out):
         dst_list = keep.tile([P, E // PER_COLUMN], U16, name="dst_list")
         src_list = keep.tile([P, E // PER_COLUMN], U16, name="src_list")
         dy = [tile([P, WIDE], F32, f"dy{t}") for t in range(PLANES)]
-        h = [tile([P, PLANES, CHUNK], F32, f"h{c}") for c in range(CHUNKS)]
+        h = {(c, u): tile([P, 2, CHUNK], F32, f"h{c}{u}") for c in range(CHUNKS) for u in range(2)}
         g = {}
-        dz = {}
+        pairs = {}
+        dz = [tile([P, CHUNK, PLANES], BF16, f"dz{c}") for c in range(CHUNKS)]
         dz_codes = [tile([P, CHUNK], U32, f"dz_codes{c}") for c in range(CHUNKS)]
         dz_scales = [tile([P, CHUNK], U8, f"dz_scales{c}") for c in range(CHUNKS)]
         w = tile([P, PLANES, D], F32, "w")
@@ -60,8 +61,9 @@ def tile_attend_gmp_kernel(tc, dyT, hE, wm, offs, offs2, out):
         def entries(offsets, a, b):
             return offsets[:, a // PER_COLUMN : b // PER_COLUMN]
 
-        def load_h(c, a=0, b=CHUNK):
-            nc.sync.dma_start(out=h[c][:, :, a:b], in_=h_planes[:, :, c * CHUNK + a : c * CHUNK + b])
+        def load_h(c):
+            for u in range(2):
+                nc.sync.dma_start(out=h[c, u][:], in_=h_planes[:, 2 * u : 2 * u + 2, edges(c)])
 
         def load_dy(t):
             nc.sync.dma_start(out=dy[t][:, :V], in_=dy_planes[:, t, :])
@@ -74,15 +76,23 @@ def tile_attend_gmp_kernel(tc, dyT, hE, wm, offs, offs2, out):
             else:
                 nc.scalar.activation(dst, picked, ACT.Copy, scale=2.0)
 
-        def make_dz(c, a, b):
+        def make_pair(c, u, a=0, b=CHUNK):
             nc.vector.scalar_tensor_tensor(
-                dz[c][:, a:b, :],
-                h[c][:, :, a:b].rearrange("p t e -> p e t"),
+                pairs[c][:, u, a:b, :],
+                h[c, u][:, :, a:b].rearrange("p t e -> p e t"),
                 0.0,
-                g[c][:, :, a:b].rearrange("p t e -> p e t"),
+                g[c][:, 2 * u : 2 * u + 2, a:b].rearrange("p t e -> p e t"),
                 ALU.max,
                 ALU.mult,
             )
+
+        def join_pairs(c, a=0, b=CHUNK):
+            src = pairs[c][:, :, a:b, :].rearrange("p u e t -> p u (e t)").bitcast(I32)
+            dst = dz[c][:, a:b, :].rearrange("p e t -> p (e t)").bitcast(I32)
+            nc.vector.tensor_copy(dst.rearrange("p (e u) -> p e u", u=2), src.rearrange("p u e -> p e u"))
+
+        def quantize_dz(c, a=0, b=CHUNK):
+            quantize(dz_codes[c][:, a:b], dz_scales[c][:, a:b], dz[c][:, a:b, :], E5M2)
 
         def round_w(copy, half, name):
             w_bf16 = tile([P, 2 * P, PLANES], BF16, name)
@@ -136,31 +146,38 @@ def tile_attend_gmp_kernel(tc, dyT, hE, wm, offs, offs2, out):
         nc.sync.dma_start(dst_list[:], offs)
         for t in range(1, PLANES):
             load_dy(t)
-        for c in (0, 1):
-            load_h(c, 0, HALF)
-            load_h(c, HALF, CHUNK)
+        load_h(0)
+        load_h(1)
         nc.sync.dma_start(out=w[:], in_=w_planes)
-        for c in (2, 3):
-            load_h(c, 0, HALF)
-            load_h(c, HALF, CHUNK)
+        load_h(2)
+        load_h(3)
         nc.sync.dma_start(src_list[:], offs2)
 
+        halves = ((0, HALF), (HALF, CHUNK))
         for c in range(CHUNKS):
             g[c] = tile([P, PLANES, CHUNK], F32, f"g{c % last_chunk}")
-            for a, b in ((0, CHUNK),) if c < last_chunk else ((0, HALF), (HALF, CHUNK)):
-                for t in range(PLANES):
-                    look_up_dy("vector" if c == 0 else "scalar", t, c, a, b)
-            dz[c] = tile([P, CHUNK, PLANES], BF16, f"dz{c}")
-            for a in (0, HALF):
-                make_dz(c, a, a + HALF)
+            for t in range(PLANES):
+                look_up_dy("vector" if c == 0 else "scalar", t, c)
+            pairs[c] = tile([P, 2, CHUNK, 2], BF16, f"pairs{min(c, 2)}")
+            make_pair(c, 0)
+            if c < last_chunk:
+                make_pair(c, 1)
             if c == 1:
-                w_bf16 = round_w(nc.vector.tensor_copy, 0, "dz2")
-            for a in (0, HALF):
-                quantize(dz_codes[c][:, a : a + HALF], dz_scales[c][:, a : a + HALF], dz[c][:, a : a + HALF, :], E5M2)
+                w_bf16 = round_w(nc.vector.tensor_copy, 0, "pairs2")
+            if c < last_chunk:
+                join_pairs(c)
             if c == 1:
                 quantize_w(0, w_bf16, "w_codes0")
-            if c == 2:
-                quantize_w(1, round_w(nc.scalar.copy, 1, "w_bf16"), "h2")
+            if c < 2:
+                quantize_dz(c)
+        quantize_dz(2)
+        quantize_w(1, round_w(nc.scalar.copy, 1, "w_bf16"), f"h{last_chunk}0")
+        for a, b in halves:
+            make_pair(last_chunk, 1, a, b)
+        for a, b in halves:
+            join_pairs(last_chunk, a, b)
+        for a, b in halves:
+            quantize_dz(last_chunk, a, b)
         for i in range(BLOCKS):
             dm[i] = tile([P, E], F32, f"dm{i}" if i < last_block else f"dz{last_chunk}")
         early = [(i, c) for c in range(last_chunk) for i in (0, 1)] + [(2, c) for c in range(last_chunk)]
@@ -173,11 +190,11 @@ def tile_attend_gmp_kernel(tc, dyT, hE, wm, offs, offs2, out):
 
         picked = {}
         for i in range(BLOCKS):
-            spans = [("vector", 0, 544), ("vector", 544, 1088), ("scalar", 1088, E)]
+            spans = [("vector", 0, 576), ("vector", 576, 1152), ("scalar", 1152, E)]
             if i == 0:
-                spans = [("vector", 0, 384), ("vector", 384, 1088), ("scalar", 1088, E)]
+                spans = [("vector", 0, 384), ("vector", 384, 1152), ("scalar", 1152, E)]
             if i == last_block:
-                spans = [("vector", 0, 1024), ("scalar", 1024, 1792), ("scalar", 1792, E)]
+                spans = [("vector", 0, 1088), ("scalar", 1088, 1792), ("scalar", 1792, E)]
             for k, (e, a, b) in enumerate(spans):
                 picked[i, k] = (a, b, look_up_dm(e, i, a, b, f"picked{i}{a}"))
             if i == 0:

@@ -18,14 +18,20 @@ ACT = mybir.ActivationFunctionType
 
 P = 128
 PLANES = 4
+PAIRS = PLANES // 2
 CHUNK = 512
 CHUNKS = E // CHUNK
 BLOCKS = D // P
+W_HALF = D // 2
 PER_COLUMN = 16
 RUN = 4
-WIDE = 2048
+WINDOW = 4 * CHUNK
 BANKS = 8
-HALF = CHUNK // 2
+
+VECTOR_SHARE = 1152
+FIRST_PIECE = 384
+LAST_VECTOR_SHARE = 1088
+LAST_PIECE = 256
 
 
 def tile_attend_gmp_kernel(tc, dyT, hE, wm, offs, offs2, out):
@@ -40,16 +46,13 @@ def tile_attend_gmp_kernel(tc, dyT, hE, wm, offs, offs2, out):
 
         dst_list = keep.tile([P, E // PER_COLUMN], U16, name="dst_list")
         src_list = keep.tile([P, E // PER_COLUMN], U16, name="src_list")
-        dy = [tile([P, WIDE], F32, f"dy{t}") for t in range(PLANES)]
-        h = {(c, u): tile([P, 2, CHUNK], F32, f"h{c}{u}") for c in range(CHUNKS) for u in range(2)}
-        g = {}
-        pairs = {}
+        dy = [tile([P, WINDOW], F32, f"dy{t}") for t in range(PLANES)]
+        h = {(c, u): tile([P, 2, CHUNK], F32, f"h{c}{u}") for c in range(CHUNKS) for u in range(PAIRS)}
         dz = [tile([P, CHUNK, PLANES], BF16, f"dz{c}") for c in range(CHUNKS)]
         dz_codes = [tile([P, CHUNK], U32, f"dz_codes{c}") for c in range(CHUNKS)]
         dz_scales = [tile([P, CHUNK], U8, f"dz_scales{c}") for c in range(CHUNKS)]
         w = tile([P, PLANES, D], F32, "w")
-        w_mx = {}
-        dm = {}
+        dy_picked, dz_pairs, w_mx = {}, {}, {}
 
         dy_planes = dyT.rearrange("(p t) v -> p t v", t=PLANES)
         h_planes = hE.rearrange("(p t) e -> p t e", t=PLANES)
@@ -58,63 +61,67 @@ def tile_attend_gmp_kernel(tc, dyT, hE, wm, offs, offs2, out):
         def edges(c):
             return slice(c * CHUNK, (c + 1) * CHUNK)
 
+        def pair(u):
+            return slice(2 * u, 2 * u + 2)
+
         def entries(offsets, a, b):
             return offsets[:, a // PER_COLUMN : b // PER_COLUMN]
-
-        def load_h(c):
-            for u in range(2):
-                nc.sync.dma_start(out=h[c, u][:], in_=h_planes[:, 2 * u : 2 * u + 2, edges(c)])
 
         def load_dy(t):
             nc.sync.dma_start(out=dy[t][:, :V], in_=dy_planes[:, t, :])
 
-        def look_up_dy(engine, t, c, a=0, b=CHUNK):
-            picked = dy[t][:].indirect(entries(dst_list, c * CHUNK + a, c * CHUNK + b))
-            dst = g[c][:, t, a:b]
-            if engine == "vector":
-                nc.vector.tensor_scalar(dst, picked, 2.0, 0.0, ALU.mult, ALU.add)
-            else:
-                nc.scalar.activation(dst, picked, ACT.Copy, scale=2.0)
+        def load_h(c):
+            for u in range(PAIRS):
+                nc.sync.dma_start(out=h[c, u][:], in_=h_planes[:, pair(u), edges(c)])
+
+        def look_up_dy(c, buffer):
+            dy_picked[c] = tile([P, PLANES, CHUNK], F32, buffer)
+            for t in range(PLANES):
+                window = dy[t][:].indirect(entries(dst_list, c * CHUNK, (c + 1) * CHUNK))
+                if c == 0:
+                    nc.vector.tensor_scalar(dy_picked[c][:, t, :], window, 2.0, 0.0, ALU.mult, ALU.add)
+                else:
+                    nc.scalar.activation(dy_picked[c][:, t, :], window, ACT.Copy, scale=2.0)
 
         def make_pair(c, u, a=0, b=CHUNK):
             nc.vector.scalar_tensor_tensor(
-                pairs[c][:, u, a:b, :],
+                dz_pairs[c][:, u, a:b, :],
                 h[c, u][:, :, a:b].rearrange("p t e -> p e t"),
                 0.0,
-                g[c][:, 2 * u : 2 * u + 2, a:b].rearrange("p t e -> p e t"),
+                dy_picked[c][:, pair(u), a:b].rearrange("p t e -> p e t"),
                 ALU.max,
                 ALU.mult,
             )
 
         def join_pairs(c, a=0, b=CHUNK):
-            src = pairs[c][:, :, a:b, :].rearrange("p u e t -> p u (e t)").bitcast(I32)
+            src = dz_pairs[c][:, :, a:b, :].rearrange("p u e t -> p u (e t)").bitcast(I32)
             dst = dz[c][:, a:b, :].rearrange("p e t -> p (e t)").bitcast(I32)
-            nc.vector.tensor_copy(dst.rearrange("p (e u) -> p e u", u=2), src.rearrange("p u e -> p e u"))
-
-        def quantize_dz(c, a=0, b=CHUNK):
-            quantize(dz_codes[c][:, a:b], dz_scales[c][:, a:b], dz[c][:, a:b, :], E5M2)
-
-        def round_w(copy, half, name):
-            w_bf16 = tile([P, 2 * P, PLANES], BF16, name)
-            columns = w[:, :, half * 2 * P : (half + 1) * 2 * P]
-            copy(w_bf16[:].rearrange("p (c i) t -> p c t i", i=RUN), columns.rearrange("p t (c i) -> p c t i", i=RUN))
-            return w_bf16
-
-        def quantize_w(half, w_bf16, name):
-            w_mx[half] = (tile([P, 2 * P], U32, name), tile([P, 2 * P], U8, f"w_scales{half}"))
-            quantize(w_mx[half][0][:], w_mx[half][1][:], w_bf16[:], E4M3)
+            nc.vector.tensor_copy(dst.rearrange("p (e u) -> p e u", u=PAIRS), src.rearrange("p u e -> p e u"))
 
         def quantize(codes, scales, values, fmt):
             nc.vector.quantize_mx(out=codes.bitcast(fmt), scales=scales, in_=values.rearrange("p c t -> p (c t)"))
 
-        def make_dm(copy, i, c, bank):
-            w_codes, w_scales = w_mx[i // 2]
-            features = slice(i % 2 * P, (i % 2 + 1) * P)
-            acc = psum.tile([P, CHUNK], F32, name=f"bank{bank}")
+        def quantize_dz(c, a=0, b=CHUNK):
+            quantize(dz_codes[c][:, a:b], dz_scales[c][:, a:b], dz[c][:, a:b, :], E5M2)
+
+        def round_w(copy, half, buffer):
+            w_bf16 = tile([P, W_HALF, PLANES], BF16, buffer)
+            columns = w[:, :, half * W_HALF : (half + 1) * W_HALF]
+            copy(w_bf16[:].rearrange("p (c i) t -> p c t i", i=RUN), columns.rearrange("p t (c i) -> p c t i", i=RUN))
+            return w_bf16
+
+        def quantize_w(half, w_bf16, buffer):
+            w_mx[half] = (tile([P, W_HALF], U32, buffer), tile([P, W_HALF], U8, f"w_scales{half}"))
+            quantize(w_mx[half][0][:], w_mx[half][1][:], w_bf16[:], E4M3)
+
+        def make_dm(copy, i, c):
+            half, first = divmod(i * P, W_HALF)
+            w_codes, w_scales = w_mx[half]
+            acc = psum.tile([P, CHUNK], F32, name=f"bank{bank[i, c]}")
             nc.tensor.matmul_mx(
                 out=acc[:],
-                lhsT=w_codes[:, features].bitcast(E4M3),
-                lhsT_scale=w_scales[:, features],
+                lhsT=w_codes[:, first : first + P].bitcast(E4M3),
+                lhsT_scale=w_scales[:, first : first + P],
                 rhs=dz_codes[c][:].bitcast(E5M2),
                 rhs_scale=dz_scales[c][:],
                 start=True,
@@ -122,26 +129,24 @@ def tile_attend_gmp_kernel(tc, dyT, hE, wm, offs, offs2, out):
             )
             copy(dm[i][:, edges(c)], acc[:])
 
-        def look_up_dm(engine, i, a, b, name):
-            picked = tile([P, b - a], F32, name)
+        def look_up_dm(i, a, b, on_vector):
+            picked = tile([P, b - a], F32, f"picked{i}{a}")
             window = dm[i][:].indirect(entries(src_list, a, b))
-            if engine == "vector":
+            if on_vector:
                 nc.vector.tensor_copy(picked[:], window)
             else:
                 nc.scalar.activation(picked[:], window, ACT.Copy)
             return picked
 
-        def add_and_store(engine, i, a, b, picked, name):
-            nodes = (b - a) // K
-            sums = tile([P, nodes], F32, name)
+        def add_and_store(i, a, b, picked):
+            engine = nc.gpsimd if i < last_block else nc.vector
+            sums = tile([P, (b - a) // K], F32, f"sums{i}{a}")
             engine.tensor_tensor(sums[:], picked[:, 0 : b - a : K], picked[:, 1 : b - a : K], ALU.add)
             nc.sync.dma_start(out=out[i * P : (i + 1) * P, a // K : b // K], in_=sums[:])
 
-        warm = tile([P, 2, 8], F32, "warm")
-        nc.gpsimd.memset(warm[:, 0, :], 0.0)
-        nc.scalar.activation(warm[:, 1, :], warm[:, 0, :], ACT.Copy)
         for t in range(PLANES):
-            (nc.vector if t < 2 else nc.gpsimd).memset(dy[t][:, V:], 0.0)
+            (nc.vector if t < PLANES // 2 else nc.gpsimd).memset(dy[t][:, V:], 0.0)
+
         load_dy(0)
         nc.sync.dma_start(dst_list[:], offs)
         for t in range(1, PLANES):
@@ -153,56 +158,64 @@ def tile_attend_gmp_kernel(tc, dyT, hE, wm, offs, offs2, out):
         load_h(3)
         nc.sync.dma_start(src_list[:], offs2)
 
-        halves = ((0, HALF), (HALF, CHUNK))
-        for c in range(CHUNKS):
-            g[c] = tile([P, PLANES, CHUNK], F32, f"g{c % last_chunk}")
-            for t in range(PLANES):
-                look_up_dy("vector" if c == 0 else "scalar", t, c)
-            pairs[c] = tile([P, 2, CHUNK, 2], BF16, f"pairs{min(c, 2)}")
+        def start_chunk(c, picked_buffer, pairs_buffer):
+            look_up_dy(c, picked_buffer)
+            dz_pairs[c] = tile([P, PAIRS, CHUNK, 2], BF16, pairs_buffer)
             make_pair(c, 0)
-            if c < last_chunk:
-                make_pair(c, 1)
-            if c == 1:
-                w_bf16 = round_w(nc.vector.tensor_copy, 0, "pairs2")
-            if c < last_chunk:
-                join_pairs(c)
-            if c == 1:
-                quantize_w(0, w_bf16, "w_codes0")
-            if c < 2:
-                quantize_dz(c)
+
+        start_chunk(0, "picked_a", "pairs_a")
+        make_pair(0, 1)
+        join_pairs(0)
+        quantize_dz(0)
+
+        start_chunk(1, "picked_b", "pairs_b")
+        make_pair(1, 1)
+        w_first_bf16 = round_w(nc.vector.tensor_copy, 0, "pairs_c")
+        join_pairs(1)
+        quantize_w(0, w_first_bf16, "w_codes0")
+        quantize_dz(1)
+
+        start_chunk(2, "picked_c", "pairs_c")
+        make_pair(2, 1)
+        join_pairs(2)
+
+        start_chunk(last_chunk, "picked_a", "pairs_c")
         quantize_dz(2)
+
         quantize_w(1, round_w(nc.scalar.copy, 1, "w_bf16"), f"h{last_chunk}0")
+
+        halves = ((0, CHUNK // 2), (CHUNK // 2, CHUNK))
         for a, b in halves:
             make_pair(last_chunk, 1, a, b)
         for a, b in halves:
             join_pairs(last_chunk, a, b)
         for a, b in halves:
             quantize_dz(last_chunk, a, b)
-        for i in range(BLOCKS):
-            dm[i] = tile([P, E], F32, f"dm{i}" if i < last_block else f"dz{last_chunk}")
-        early = [(i, c) for c in range(last_chunk) for i in (0, 1)] + [(2, c) for c in range(last_chunk)]
-        for n, (i, c) in enumerate(early):
-            make_dm(nc.scalar.copy, i, c, n % BANKS)
-        make_dm(nc.vector.tensor_copy, last_block, 0, 1)
-        make_dm(nc.scalar.copy, last_block, 1, 2)
-        make_dm(nc.vector.tensor_copy, 0, last_chunk, 3)
-        make_dm(nc.scalar.copy, 1, last_chunk, 4)
 
-        picked = {}
+        dm = [tile([P, E], F32, f"dm{i}" if i < last_block else f"dz{last_chunk}") for i in range(BLOCKS)]
+        early = [(i, c) for c in range(last_chunk) for i in (0, 1)] + [(2, c) for c in range(last_chunk)]
+        in_turn = early + [(last_block, 0), (last_block, 1)] + [(i, last_chunk) for i in range(BLOCKS)]
+        bank = {key: n % BANKS for n, key in enumerate(in_turn)}
+        bank[last_block, 2] = bank[0, last_chunk]
+        for i, c in early:
+            make_dm(nc.scalar.copy, i, c)
+        make_dm(nc.vector.tensor_copy, last_block, 0)
+        make_dm(nc.scalar.copy, last_block, 1)
+        make_dm(nc.vector.tensor_copy, 0, last_chunk)
+        make_dm(nc.scalar.copy, 1, last_chunk)
+
+        left = {0: [(2, last_chunk)], 1: [(last_block, 2), (last_block, last_chunk)]}
+        pieces = []
         for i in range(BLOCKS):
-            spans = [("vector", 0, 576), ("vector", 576, 1152), ("scalar", 1152, E)]
-            if i == 0:
-                spans = [("vector", 0, 384), ("vector", 384, 1152), ("scalar", 1152, E)]
-            if i == last_block:
-                spans = [("vector", 0, 1088), ("scalar", 1088, 1792), ("scalar", 1792, E)]
-            for k, (e, a, b) in enumerate(spans):
-                picked[i, k] = (a, b, look_up_dm(e, i, a, b, f"picked{i}{a}"))
-            if i == 0:
-                make_dm(nc.scalar.copy, 2, last_chunk, 5)
-            if i == 1:
-                make_dm(nc.scalar.copy, last_block, 2, 3)
-                make_dm(nc.scalar.copy, last_block, last_chunk, 6)
-        order = [(0, 0), (0, 1), (0, 2), (1, 0), (1, 1), (1, 2), (2, 0), (2, 1), (2, 2), (3, 0), (3, 1), (3, 2)]
-        for n, (i, k) in enumerate(order):
-            a, b, columns = picked[i, k]
-            add_and_store(nc.gpsimd if n < len(order) - 3 else nc.vector, i, a, b, columns, f"sums{i}{a}")
+            if i < last_block:
+                share = VECTOR_SHARE
+                cuts = (0, FIRST_PIECE if i == 0 else share // 2, share, E)
+            else:
+                share = LAST_VECTOR_SHARE
+                cuts = (0, share, E - LAST_PIECE, E)
+            for a, b in zip(cuts, cuts[1:]):
+                pieces.append((i, a, b, look_up_dm(i, a, b, a < share)))
+            for block, c in left.get(i, []):
+                make_dm(nc.scalar.copy, block, c)
+        for piece in pieces:
+            add_and_store(*piece)

@@ -20,18 +20,14 @@ P = 128
 PLANES = 4
 PAIRS = PLANES // 2
 CHUNK = 512
+HALF = CHUNK // 2
 CHUNKS = E // CHUNK
 BLOCKS = D // P
-W_HALF = D // 2
 PER_COLUMN = 16
-RUN = 4
 WINDOW = 4 * CHUNK
-BANKS = 8
 
-VECTOR_SHARE = 1152
-FIRST_PIECE = 384
-LAST_VECTOR_SHARE = 1088
-LAST_PIECE = 256
+CUTS = (0, 544, 1024, 1568, E)
+LAST_CUTS = (0, 512, 1152, 1600, E)
 
 
 def tile_attend_gmp_kernel(tc, dyT, hE, wm, offs, offs2, out):
@@ -51,15 +47,19 @@ def tile_attend_gmp_kernel(tc, dyT, hE, wm, offs, offs2, out):
         dz = [tile([P, CHUNK, PLANES], BF16, f"dz{c}") for c in range(CHUNKS)]
         dz_codes = [tile([P, CHUNK], U32, f"dz_codes{c}") for c in range(CHUNKS)]
         dz_scales = [tile([P, CHUNK], U8, f"dz_scales{c}") for c in range(CHUNKS)]
+        dz_pairs = [tile([P, PAIRS, CHUNK, 2], BF16, f"pairs{c}") for c in range(CHUNKS)]
         w = tile([P, PLANES, D], F32, "w")
-        dy_picked, dz_pairs, w_mx = {}, {}, {}
+        w_bf16 = tile([P, D, PLANES], BF16, "w_bf16")
+        w_scales = tile([P, D], U8, "w_scales")
+        dm = [tile([P, E], F32, f"dm{i}") for i in range(BLOCKS)]
+        dy_picked = {}
 
         dy_planes = dyT.rearrange("(p t) v -> p t v", t=PLANES)
         h_planes = hE.rearrange("(p t) e -> p t e", t=PLANES)
         w_planes = wm.rearrange("(p t) d -> p t d", t=PLANES)
 
-        def edges(c):
-            return slice(c * CHUNK, (c + 1) * CHUNK)
+        def edges(c, a=0, b=CHUNK):
+            return slice(c * CHUNK + a, c * CHUNK + b)
 
         def pair(u):
             return slice(2 * u, 2 * u + 2)
@@ -70,33 +70,30 @@ def tile_attend_gmp_kernel(tc, dyT, hE, wm, offs, offs2, out):
         def load_dy(t):
             nc.sync.dma_start(out=dy[t][:, :V], in_=dy_planes[:, t, :])
 
-        def load_h(c):
-            for u in range(PAIRS):
-                nc.sync.dma_start(out=h[c, u][:], in_=h_planes[:, pair(u), edges(c)])
-
-        def look_up_dy(c, buffer):
-            dy_picked[c] = tile([P, PLANES, CHUNK], F32, buffer)
-            for t in range(PLANES):
-                window = dy[t][:].indirect(entries(dst_list, c * CHUNK, (c + 1) * CHUNK))
-                if c == 0:
-                    nc.vector.tensor_scalar(dy_picked[c][:, t, :], window, 2.0, 0.0, ALU.mult, ALU.add)
-                else:
-                    nc.scalar.activation(dy_picked[c][:, t, :], window, ACT.Copy, scale=2.0)
+        def look_up_dy(c, t, on_vector, buffer=None):
+            u = t // 2
+            if (c, u) not in dy_picked:
+                dy_picked[c, u] = tile([P, 2, CHUNK], F32, buffer or f"picked_dy{c}{u}")
+            window = dy[t][:].indirect(entries(dst_list, c * CHUNK, (c + 1) * CHUNK))
+            if on_vector:
+                nc.vector.tensor_scalar(dy_picked[c, u][:, t % 2, :], window, 2.0, 0.0, ALU.mult, ALU.add)
+            else:
+                nc.scalar.activation(dy_picked[c, u][:, t % 2, :], window, ACT.Copy, scale=2.0)
 
         def make_pair(c, u, a=0, b=CHUNK):
             nc.vector.scalar_tensor_tensor(
                 dz_pairs[c][:, u, a:b, :],
                 h[c, u][:, :, a:b].rearrange("p t e -> p e t"),
                 0.0,
-                dy_picked[c][:, pair(u), a:b].rearrange("p t e -> p e t"),
+                dy_picked[c, u][:, :, a:b].rearrange("p t e -> p e t"),
                 ALU.max,
                 ALU.mult,
             )
 
-        def join_pairs(c, a=0, b=CHUNK):
-            src = dz_pairs[c][:, :, a:b, :].rearrange("p u e t -> p u (e t)").bitcast(I32)
-            dst = dz[c][:, a:b, :].rearrange("p e t -> p (e t)").bitcast(I32)
-            nc.vector.tensor_copy(dst.rearrange("p (e u) -> p e u", u=PAIRS), src.rearrange("p u e -> p e u"))
+        def join_pairs(c, copy, word, a=0, b=CHUNK):
+            src = dz_pairs[c][:, :, a:b, :].rearrange("p u e t -> p u (e t)").bitcast(word)
+            dst = dz[c][:, a:b, :].rearrange("p e t -> p (e t)").bitcast(word)
+            copy(dst.rearrange("p (e u) -> p e u", u=PAIRS), src.rearrange("p u e -> p e u"))
 
         def quantize(codes, scales, values, fmt):
             nc.vector.quantize_mx(out=codes.bitcast(fmt), scales=scales, in_=values.rearrange("p c t -> p (c t)"))
@@ -104,118 +101,108 @@ def tile_attend_gmp_kernel(tc, dyT, hE, wm, offs, offs2, out):
         def quantize_dz(c, a=0, b=CHUNK):
             quantize(dz_codes[c][:, a:b], dz_scales[c][:, a:b], dz[c][:, a:b, :], E5M2)
 
-        def round_w(copy, half, buffer):
-            w_bf16 = tile([P, W_HALF, PLANES], BF16, buffer)
-            columns = w[:, :, half * W_HALF : (half + 1) * W_HALF]
-            copy(w_bf16[:].rearrange("p (c i) t -> p c t i", i=RUN), columns.rearrange("p t (c i) -> p c t i", i=RUN))
-            return w_bf16
-
-        def quantize_w(half, w_bf16, buffer):
-            w_mx[half] = (tile([P, W_HALF], U32, buffer), tile([P, W_HALF], U8, f"w_scales{half}"))
-            quantize(w_mx[half][0][:], w_mx[half][1][:], w_bf16[:], E4M3)
-
-        def make_dm(copy, i, c):
-            half, first = divmod(i * P, W_HALF)
-            w_codes, w_scales = w_mx[half]
-            acc = psum.tile([P, CHUNK], F32, name=f"bank{bank[i, c]}")
+        def make_dm(copy, bank, i, c, a=0, b=CHUNK):
+            acc = psum.tile([P, b - a], F32, name=f"bank{bank}")
             nc.tensor.matmul_mx(
                 out=acc[:],
-                lhsT=w_codes[:, first : first + P].bitcast(E4M3),
-                lhsT_scale=w_scales[:, first : first + P],
-                rhs=dz_codes[c][:].bitcast(E5M2),
-                rhs_scale=dz_scales[c][:],
+                lhsT=w_codes[:, i * P : (i + 1) * P].bitcast(E4M3),
+                lhsT_scale=w_scales[:, i * P : (i + 1) * P],
+                rhs=dz_codes[c][:, a:b].bitcast(E5M2),
+                rhs_scale=dz_scales[c][:, a:b],
                 start=True,
                 stop=True,
             )
-            copy(dm[i][:, edges(c)], acc[:])
+            copy(dm[i][:, edges(c, a, b)], acc[:])
 
-        def look_up_dm(i, a, b, on_vector):
-            picked = tile([P, b - a], F32, f"picked{i}{a}")
-            window = dm[i][:].indirect(entries(src_list, a, b))
-            if on_vector:
-                nc.vector.tensor_copy(picked[:], window)
-            else:
-                nc.scalar.activation(picked[:], window, ACT.Copy)
-            return picked
+        def look_up_add_store(engine, pieces, name):
+            width = sum(b - a for i, a, b, on_vector in pieces)
+            picked = tile([P, width], F32, f"picked_dm{name}")
+            sums = tile([P, width // K], F32, f"sums{name}")
+            at = 0
+            for i, a, b, on_vector in pieces:
+                window = dm[i][:].indirect(entries(src_list, a, b))
+                if on_vector:
+                    nc.vector.tensor_copy(picked[:, at : at + b - a], window)
+                else:
+                    nc.scalar.activation(picked[:, at : at + b - a], window, ACT.Copy)
+                at = at + b - a
+            engine.tensor_tensor(sums[:], picked[:, 0:width:K], picked[:, 1:width:K], ALU.add)
+            if pieces[0][0] == pieces[-1][0]:
+                pieces = [(pieces[0][0], pieces[0][1], pieces[-1][2], None)]
+            at = 0
+            for i, a, b, on_vector in pieces:
+                nc.sync.dma_start(out=out[i * P : (i + 1) * P, a // K : b // K], in_=sums[:, at // K : (at + b - a) // K])
+                at = at + b - a
 
-        def add_and_store(i, a, b, picked):
-            engine = nc.gpsimd if i < last_block else nc.vector
-            sums = tile([P, (b - a) // K], F32, f"sums{i}{a}")
-            engine.tensor_tensor(sums[:], picked[:, 0 : b - a : K], picked[:, 1 : b - a : K], ALU.add)
-            nc.sync.dma_start(out=out[i * P : (i + 1) * P, a // K : b // K], in_=sums[:])
+        warm_in = tile([P, 1], F32, "warm_in")
+        warm_out = tile([P, 1], F32, "warm_out")
+        nc.gpsimd.memset(warm_in[:], 0.0)
+        nc.scalar.activation(warm_out[:], warm_in[:], ACT.Copy)
 
         for t in range(PLANES):
             (nc.vector if t < PLANES // 2 else nc.gpsimd).memset(dy[t][:, V:], 0.0)
 
         load_dy(0)
         nc.sync.dma_start(dst_list[:], offs)
-        for t in range(1, PLANES):
-            load_dy(t)
-        load_h(0)
-        load_h(1)
+        load_dy(1)
         nc.sync.dma_start(out=w[:], in_=w_planes)
-        load_h(2)
-        load_h(3)
+        load_dy(2)
+        load_dy(3)
+        for c in range(CHUNKS):
+            for u in range(PAIRS):
+                nc.sync.dma_start(out=h[c, u][:], in_=h_planes[:, pair(u), edges(c)])
         nc.sync.dma_start(src_list[:], offs2)
 
-        def start_chunk(c, picked_buffer, pairs_buffer):
-            look_up_dy(c, picked_buffer)
-            dz_pairs[c] = tile([P, PAIRS, CHUNK, 2], BF16, pairs_buffer)
-            make_pair(c, 0)
+        for t in range(2):
+            for c in range(CHUNKS):
+                look_up_dy(c, t, c < 2)
+        for half in range(2):
+            columns = slice(half * (D // 2), (half + 1) * (D // 2))
+            nc.gpsimd.tensor_copy(w_bf16[:, columns, :], w[:, :, columns].rearrange("p t c -> p c t"))
+        for c in range(last_chunk):
+            for t in range(2, PLANES):
+                look_up_dy(c, t, c == 0)
 
-        start_chunk(0, "picked_a", "pairs_a")
+        make_pair(0, 0)
         make_pair(0, 1)
-        join_pairs(0)
-        quantize_dz(0)
-
-        start_chunk(1, "picked_b", "pairs_b")
+        w_codes = tile([P, D], U32, "h00")
+        quantize(w_codes[:], w_scales[:], w_bf16[:], E4M3)
+        join_pairs(0, nc.scalar.copy, U32)
+        for t in range(2, PLANES):
+            look_up_dy(last_chunk, t, False, "pairs0")
+        make_pair(1, 0)
         make_pair(1, 1)
-        w_first_bf16 = round_w(nc.vector.tensor_copy, 0, "pairs_c")
-        join_pairs(1)
-        quantize_w(0, w_first_bf16, "w_codes0")
-        quantize_dz(1)
-
-        start_chunk(2, "picked_c", "pairs_c")
+        quantize_dz(0)
+        join_pairs(1, nc.scalar.copy, U32)
+        make_pair(2, 0)
         make_pair(2, 1)
-        join_pairs(2)
-
-        start_chunk(last_chunk, "picked_a", "pairs_c")
+        quantize_dz(1)
+        join_pairs(2, nc.vector.tensor_copy, I32)
+        make_pair(last_chunk, 0)
         quantize_dz(2)
-
-        quantize_w(1, round_w(nc.scalar.copy, 1, "w_bf16"), f"h{last_chunk}0")
-
-        halves = ((0, CHUNK // 2), (CHUNK // 2, CHUNK))
+        halves = ((0, HALF), (HALF, CHUNK))
         for a, b in halves:
             make_pair(last_chunk, 1, a, b)
         for a, b in halves:
-            join_pairs(last_chunk, a, b)
+            join_pairs(last_chunk, nc.vector.tensor_copy, I32, a, b)
         for a, b in halves:
             quantize_dz(last_chunk, a, b)
 
-        dm = [tile([P, E], F32, f"dm{i}" if i < last_block else f"dz{last_chunk}") for i in range(BLOCKS)]
-        early = [(i, c) for c in range(last_chunk) for i in (0, 1)] + [(2, c) for c in range(last_chunk)]
-        in_turn = early + [(last_block, 0), (last_block, 1)] + [(i, last_chunk) for i in range(BLOCKS)]
-        bank = {key: n % BANKS for n, key in enumerate(in_turn)}
-        bank[last_block, 2] = bank[0, last_chunk]
-        for i, c in early:
-            make_dm(nc.scalar.copy, i, c)
-        make_dm(nc.vector.tensor_copy, last_block, 0)
-        make_dm(nc.scalar.copy, last_block, 1)
-        make_dm(nc.vector.tensor_copy, 0, last_chunk)
-        make_dm(nc.scalar.copy, 1, last_chunk)
+        for c in range(last_chunk):
+            for i in range(BLOCKS):
+                late = (i, c) == (last_block, last_chunk - 1)
+                make_dm(nc.vector.tensor_copy if late else nc.scalar.copy, (c % 2) * BLOCKS + i, i, c)
+        make_dm(nc.scalar.copy, 4, 0, last_chunk, 0, HALF)
+        make_dm(nc.vector.tensor_copy, 5, 0, last_chunk, HALF, CHUNK)
+        make_dm(nc.scalar.copy, 6, 1, last_chunk)
 
-        left = {0: [(2, last_chunk)], 1: [(last_block, 2), (last_block, last_chunk)]}
+        make_dm(nc.scalar.copy, 7, 2, last_chunk)
+        make_dm(nc.scalar.copy, 0, last_block, last_chunk)
+
         pieces = []
         for i in range(BLOCKS):
-            if i < last_block:
-                share = VECTOR_SHARE
-                cuts = (0, FIRST_PIECE if i == 0 else share // 2, share, E)
-            else:
-                share = LAST_VECTOR_SHARE
-                cuts = (0, share, E - LAST_PIECE, E)
-            for a, b in zip(cuts, cuts[1:]):
-                pieces.append((i, a, b, look_up_dm(i, a, b, a < share)))
-            for block, c in left.get(i, []):
-                make_dm(nc.scalar.copy, block, c)
-        for piece in pieces:
-            add_and_store(*piece)
+            cuts = CUTS if i < last_block else LAST_CUTS
+            pieces.extend((i, a, b, n % 2 == 0) for n, (a, b) in enumerate(zip(cuts, cuts[1:])))
+        groups = [pieces[:1]] + [pieces[n : n + 2] for n in range(1, len(pieces), 2)]
+        for n, group in enumerate(groups):
+            look_up_add_store(nc.gpsimd if n < len(groups) - 2 else nc.vector, group, n)

@@ -144,36 +144,33 @@ def tile_attend_gmp_kernel(tc, dyT, hE, wm, offs, offs2, out):
 
         load_dy(0)
         nc.sync.dma_start(dst_list[:], offs)
-        load_dy(1)
-        nc.sync.dma_start(out=w[:], in_=w_planes)
-        load_dy(2)
-        load_dy(3)
+        for t in range(1, PLANES):
+            load_dy(t)
         for c in range(CHUNKS):
             for u in range(PAIRS):
                 nc.sync.dma_start(out=h[c, u][:], in_=h_planes[:, pair(u), edges(c)])
+            if c == 1:
+                nc.sync.dma_start(out=w[:], in_=w_planes)
         nc.sync.dma_start(src_list[:], offs2)
 
-        for t in range(2):
-            for c in range(CHUNKS):
-                look_up_dy(c, t, c < 2)
-        for half in range(2):
-            columns = slice(half * (D // 2), (half + 1) * (D // 2))
-            nc.gpsimd.tensor_copy(w_bf16[:, columns, :], w[:, :, columns].rearrange("p t c -> p c t"))
         for c in range(last_chunk):
-            for t in range(2, PLANES):
+            for t in range(PLANES):
                 look_up_dy(c, t, c == 0)
 
         make_pair(0, 0)
         make_pair(0, 1)
-        w_codes = tile([P, D], U32, "h00")
-        quantize(w_codes[:], w_scales[:], w_bf16[:], E4M3)
-        join_pairs(0, nc.scalar.copy, U32)
-        for t in range(2, PLANES):
-            look_up_dy(last_chunk, t, False, "pairs0")
+        for t in range(PLANES):
+            look_up_dy(last_chunk, t, False, f"picked_dy0{t // 2}")
         make_pair(1, 0)
+        join_pairs(0, nc.vector.tensor_copy, I32)
         make_pair(1, 1)
         quantize_dz(0)
-        join_pairs(1, nc.scalar.copy, U32)
+        nc.vector.tensor_copy(
+            w_bf16[:].rearrange("p (c i) t -> p c t i", i=4), w[:].rearrange("p t (c i) -> p c t i", i=4)
+        )
+        join_pairs(1, nc.vector.tensor_copy, I32)
+        w_codes = tile([P, D], U32, "w_codes")
+        quantize(w_codes[:], w_scales[:], w_bf16[:], E4M3)
         make_pair(2, 0)
         make_pair(2, 1)
         quantize_dz(1)

@@ -26,8 +26,9 @@ BLOCKS = D // P
 PER_COLUMN = 16
 WINDOW = 4 * CHUNK
 
-CUTS = (0, 544, 1024, 1568, E)
-LAST_CUTS = (0, 512, 1152, 1600, E)
+PIECE = E // 4
+LAST_VECTOR = 1152
+LAST_PIECE = 384
 
 
 def tile_attend_gmp_kernel(tc, dyT, hE, wm, offs, offs2, out):
@@ -114,10 +115,8 @@ def tile_attend_gmp_kernel(tc, dyT, hE, wm, offs, offs2, out):
             )
             copy(dm[i][:, edges(c, a, b)], acc[:])
 
-        def look_up_add_store(engine, pieces, name):
-            width = sum(b - a for i, a, b, on_vector in pieces)
-            picked = tile([P, width], F32, f"picked_dm{name}")
-            sums = tile([P, width // K], F32, f"sums{name}")
+        def look_up_dm(pieces, name):
+            picked = tile([P, sum(b - a for i, a, b, on_vector in pieces)], F32, f"picked_dm{name}")
             at = 0
             for i, a, b, on_vector in pieces:
                 window = dm[i][:].indirect(entries(src_list, a, b))
@@ -126,11 +125,14 @@ def tile_attend_gmp_kernel(tc, dyT, hE, wm, offs, offs2, out):
                 else:
                     nc.scalar.activation(picked[:, at : at + b - a], window, ACT.Copy)
                 at = at + b - a
+            return picked
+
+        def add_and_store(engine, picked, runs, name):
+            width = sum(b - a for i, a, b in runs)
+            sums = tile([P, width // K], F32, f"sums{name}")
             engine.tensor_tensor(sums[:], picked[:, 0:width:K], picked[:, 1:width:K], ALU.add)
-            if pieces[0][0] == pieces[-1][0]:
-                pieces = [(pieces[0][0], pieces[0][1], pieces[-1][2], None)]
             at = 0
-            for i, a, b, on_vector in pieces:
+            for i, a, b in runs:
                 nc.sync.dma_start(out=out[i * P : (i + 1) * P, a // K : b // K], in_=sums[:, at // K : (at + b - a) // K])
                 at = at + b - a
 
@@ -196,10 +198,18 @@ def tile_attend_gmp_kernel(tc, dyT, hE, wm, offs, offs2, out):
         make_dm(nc.scalar.copy, 7, 2, last_chunk)
         make_dm(nc.scalar.copy, 0, last_block, last_chunk)
 
-        pieces = []
-        for i in range(BLOCKS):
-            cuts = CUTS if i < last_block else LAST_CUTS
-            pieces.extend((i, a, b, n % 2 == 0) for n, (a, b) in enumerate(zip(cuts, cuts[1:])))
+        pieces = [(i, a, a + PIECE, a % (2 * PIECE) == 0) for i in range(last_block) for a in range(0, E, PIECE)]
         groups = [pieces[:1]] + [pieces[n : n + 2] for n in range(1, len(pieces), 2)]
         for n, group in enumerate(groups):
-            look_up_add_store(nc.gpsimd if n < len(groups) - 2 else nc.vector, group, n)
+            picked = look_up_dm(group, n)
+            (i, a, b), (j, c, d) = group[0][:3], group[-1][:3]
+            add_and_store(nc.gpsimd, picked[:], [(i, a, d)] if i == j else [(i, a, b), (j, c, d)], n)
+
+        middle, late = LAST_VECTOR // 2, E - LAST_PIECE
+        by_vector = look_up_dm([(last_block, 0, LAST_VECTOR, True)], "v")
+        by_scalar = look_up_dm([(last_block, LAST_VECTOR, late, False)], "s")
+        by_scalar_late = look_up_dm([(last_block, late, E, False)], "t")
+        add_and_store(nc.vector, by_scalar[:], [(last_block, LAST_VECTOR, late)], "s")
+        add_and_store(nc.vector, by_vector[:, :middle], [(last_block, 0, middle)], "u")
+        add_and_store(nc.vector, by_vector[:, middle:], [(last_block, middle, LAST_VECTOR)], "v")
+        add_and_store(nc.vector, by_scalar_late[:], [(last_block, late, E)], "t")

@@ -53,6 +53,7 @@ def tile_attend_gmp_kernel(tc, dyT, hE, wm, offs, offs2, out):
         w_bf16 = tile([P, D, PLANES], BF16, "w_bf16")
         w_scales = tile([P, D], U8, "w_scales")
         dm = [tile([P, E], F32, f"dm{i}") for i in range(BLOCKS)]
+        sums = tile([P, BLOCKS * V], F32, "sums")
         dy_picked = {}
 
         dy_planes = dyT.rearrange("(p t) v -> p t v", t=PLANES)
@@ -127,14 +128,12 @@ def tile_attend_gmp_kernel(tc, dyT, hE, wm, offs, offs2, out):
                 at = at + b - a
             return picked
 
-        def add_and_store(engine, picked, runs, name):
-            width = sum(b - a for i, a, b in runs)
-            sums = tile([P, width // K], F32, f"sums{name}")
-            engine.tensor_tensor(sums[:], picked[:, 0:width:K], picked[:, 1:width:K], ALU.add)
-            at = 0
-            for i, a, b in runs:
-                nc.sync.dma_start(out=out[i * P : (i + 1) * P, a // K : b // K], in_=sums[:, at // K : (at + b - a) // K])
-                at = at + b - a
+        def add(engine, picked, first, end):
+            width = end - first
+            engine.tensor_tensor(sums[:, first // K : end // K], picked[:, 0:width:K], picked[:, 1:width:K], ALU.add)
+
+        def store(i, a, b):
+            nc.sync.dma_start(out=out[i * P : (i + 1) * P, a // K : b // K], in_=sums[:, (i * E + a) // K : (i * E + b) // K])
 
         warm_in = tile([P, 1], F32, "warm_in")
         warm_out = tile([P, 1], F32, "warm_out")
@@ -202,14 +201,24 @@ def tile_attend_gmp_kernel(tc, dyT, hE, wm, offs, offs2, out):
         groups = [pieces[:1]] + [pieces[n : n + 2] for n in range(1, len(pieces), 2)]
         for n, group in enumerate(groups):
             picked = look_up_dm(group, n)
-            (i, a, b), (j, c, d) = group[0][:3], group[-1][:3]
-            add_and_store(nc.gpsimd, picked[:], [(i, a, d)] if i == j else [(i, a, b), (j, c, d)], n)
+            (i, a), (j, d) = group[0][:2], (group[-1][0], group[-1][2])
+            add(nc.gpsimd, picked[:], i * E + a, j * E + d)
+            if a == PIECE:
+                store(i, 0 if i < last_block - 1 else PIECE, 3 * PIECE)
+            if a == 3 * PIECE:
+                store(i, a, E)
+                if j == last_block - 1 > i:
+                    store(j, 0, PIECE)
 
-        middle, late = LAST_VECTOR // 2, E - LAST_PIECE
+        middle, late, start = LAST_VECTOR // 2, E - LAST_PIECE, last_block * E
         by_vector = look_up_dm([(last_block, 0, LAST_VECTOR, True)], "v")
         by_scalar = look_up_dm([(last_block, LAST_VECTOR, late, False)], "s")
         by_scalar_late = look_up_dm([(last_block, late, E, False)], "t")
-        add_and_store(nc.vector, by_scalar[:], [(last_block, LAST_VECTOR, late)], "s")
-        add_and_store(nc.vector, by_vector[:, :middle], [(last_block, 0, middle)], "u")
-        add_and_store(nc.vector, by_vector[:, middle:], [(last_block, middle, LAST_VECTOR)], "v")
-        add_and_store(nc.vector, by_scalar_late[:], [(last_block, late, E)], "t")
+        for picked, a, b in (
+            (by_vector[:, :middle], 0, middle),
+            (by_vector[:, middle:], middle, LAST_VECTOR),
+            (by_scalar[:], LAST_VECTOR, late),
+            (by_scalar_late[:], late, E),
+        ):
+            add(nc.vector, picked, start + a, start + b)
+            store(last_block, a, b)

@@ -24,10 +24,12 @@ HALF = CHUNK // 2
 CHUNKS = E // CHUNK
 BLOCKS = D // P
 PER_COLUMN = 16
+RUN = 4
 WINDOW = 4 * CHUNK
 
 PIECE = E // 4
-LAST_VECTOR = 1152
+LONG_PIECE = PIECE + 128
+LAST_VECTOR = 1024
 LAST_PIECE = 384
 
 
@@ -63,24 +65,21 @@ def tile_attend_gmp_kernel(tc, dyT, hE, wm, offs, offs2, out):
         def edges(c, a=0, b=CHUNK):
             return slice(c * CHUNK + a, c * CHUNK + b)
 
-        def pair(u):
-            return slice(2 * u, 2 * u + 2)
-
         def entries(offsets, a, b):
             return offsets[:, a // PER_COLUMN : b // PER_COLUMN]
 
         def load_dy(t):
             nc.sync.dma_start(out=dy[t][:, :V], in_=dy_planes[:, t, :])
 
-        def look_up_dy(c, t, on_vector, buffer=None):
-            u = t // 2
-            if (c, u) not in dy_picked:
-                dy_picked[c, u] = tile([P, 2, CHUNK], F32, buffer or f"picked_dy{c}{u}")
-            window = dy[t][:].indirect(entries(dst_list, c * CHUNK, (c + 1) * CHUNK))
-            if on_vector:
-                nc.vector.tensor_scalar(dy_picked[c, u][:, t % 2, :], window, 2.0, 0.0, ALU.mult, ALU.add)
-            else:
-                nc.scalar.activation(dy_picked[c, u][:, t % 2, :], window, ACT.Copy, scale=2.0)
+        def look_up_dy(c, buffer):
+            for u in range(PAIRS):
+                dy_picked[c, u] = tile([P, 2, CHUNK], F32, f"{buffer}{u}")
+                for t in range(2):
+                    window = dy[2 * u + t][:].indirect(entries(dst_list, c * CHUNK, (c + 1) * CHUNK))
+                    if c == 0:
+                        nc.vector.tensor_scalar(dy_picked[c, u][:, t, :], window, 2.0, 0.0, ALU.mult, ALU.add)
+                    else:
+                        nc.scalar.activation(dy_picked[c, u][:, t, :], window, ACT.Copy, scale=2.0)
 
         def make_pair(c, u, a=0, b=CHUNK):
             nc.vector.scalar_tensor_tensor(
@@ -92,10 +91,10 @@ def tile_attend_gmp_kernel(tc, dyT, hE, wm, offs, offs2, out):
                 ALU.mult,
             )
 
-        def join_pairs(c, copy, word, a=0, b=CHUNK):
-            src = dz_pairs[c][:, :, a:b, :].rearrange("p u e t -> p u (e t)").bitcast(word)
-            dst = dz[c][:, a:b, :].rearrange("p e t -> p (e t)").bitcast(word)
-            copy(dst.rearrange("p (e u) -> p e u", u=PAIRS), src.rearrange("p u e -> p e u"))
+        def join_pairs(c, a=0, b=CHUNK):
+            src = dz_pairs[c][:, :, a:b, :].rearrange("p u e t -> p u (e t)").bitcast(I32)
+            dst = dz[c][:, a:b, :].rearrange("p e t -> p (e t)").bitcast(I32)
+            nc.vector.tensor_copy(dst.rearrange("p (e u) -> p e u", u=PAIRS), src.rearrange("p u e -> p e u"))
 
         def quantize(codes, scales, values, fmt):
             nc.vector.quantize_mx(out=codes.bitcast(fmt), scales=scales, in_=values.rearrange("p c t -> p (c t)"))
@@ -149,76 +148,78 @@ def tile_attend_gmp_kernel(tc, dyT, hE, wm, offs, offs2, out):
             load_dy(t)
         for c in range(CHUNKS):
             for u in range(PAIRS):
-                nc.sync.dma_start(out=h[c, u][:], in_=h_planes[:, pair(u), edges(c)])
+                nc.sync.dma_start(out=h[c, u][:], in_=h_planes[:, 2 * u : 2 * u + 2, edges(c)])
             if c == 1:
                 nc.sync.dma_start(out=w[:], in_=w_planes)
         nc.sync.dma_start(src_list[:], offs2)
 
         for c in range(last_chunk):
-            for t in range(PLANES):
-                look_up_dy(c, t, c == 0)
-
+            look_up_dy(c, f"picked_dy{c}")
         make_pair(0, 0)
         make_pair(0, 1)
-        for t in range(PLANES):
-            look_up_dy(last_chunk, t, False, f"picked_dy0{t // 2}")
+        look_up_dy(last_chunk, "picked_dy0")
+
         make_pair(1, 0)
-        join_pairs(0, nc.vector.tensor_copy, I32)
+        join_pairs(0)
         make_pair(1, 1)
         quantize_dz(0)
         nc.vector.tensor_copy(
-            w_bf16[:].rearrange("p (c i) t -> p c t i", i=4), w[:].rearrange("p t (c i) -> p c t i", i=4)
+            w_bf16[:].rearrange("p (c i) t -> p c t i", i=RUN), w[:].rearrange("p t (c i) -> p c t i", i=RUN)
         )
-        join_pairs(1, nc.vector.tensor_copy, I32)
+        join_pairs(1)
         w_codes = tile([P, D], U32, "w_codes")
         quantize(w_codes[:], w_scales[:], w_bf16[:], E4M3)
         make_pair(2, 0)
         make_pair(2, 1)
         quantize_dz(1)
-        join_pairs(2, nc.vector.tensor_copy, I32)
+        join_pairs(2)
         make_pair(last_chunk, 0)
         quantize_dz(2)
         halves = ((0, HALF), (HALF, CHUNK))
         for a, b in halves:
             make_pair(last_chunk, 1, a, b)
         for a, b in halves:
-            join_pairs(last_chunk, nc.vector.tensor_copy, I32, a, b)
+            join_pairs(last_chunk, a, b)
         for a, b in halves:
             quantize_dz(last_chunk, a, b)
 
         for c in range(last_chunk):
             for i in range(BLOCKS):
-                late = (i, c) == (last_block, last_chunk - 1)
-                make_dm(nc.vector.tensor_copy if late else nc.scalar.copy, (c % 2) * BLOCKS + i, i, c)
-        make_dm(nc.scalar.copy, 4, 0, last_chunk, 0, HALF)
-        make_dm(nc.vector.tensor_copy, 5, 0, last_chunk, HALF, CHUNK)
-        make_dm(nc.scalar.copy, 6, 1, last_chunk)
+                on_vector = (i, c) == (last_block, last_chunk - 1)
+                make_dm(nc.vector.tensor_copy if on_vector else nc.scalar.copy, (c % 2) * BLOCKS + i, i, c)
+        make_dm(nc.scalar.copy, BLOCKS, 0, last_chunk, 0, HALF)
+        make_dm(nc.vector.tensor_copy, BLOCKS + 1, 0, last_chunk, HALF, CHUNK)
+        for i in range(1, BLOCKS):
+            make_dm(nc.scalar.copy, (BLOCKS + 1 + i) % (2 * BLOCKS), i, last_chunk)
 
-        make_dm(nc.scalar.copy, 7, 2, last_chunk)
-        make_dm(nc.scalar.copy, 0, last_block, last_chunk)
-
-        pieces = [(i, a, a + PIECE, a % (2 * PIECE) == 0) for i in range(last_block) for a in range(0, E, PIECE)]
+        pieces = []
+        for i in range(last_block):
+            cuts = (0, PIECE, 2 * PIECE, 2 * PIECE + (PIECE if i < last_block - 1 else LONG_PIECE), E)
+            pieces.extend((i, a, b, n % 2 == 0) for n, (a, b) in enumerate(zip(cuts, cuts[1:])))
         groups = [pieces[:1]] + [pieces[n : n + 2] for n in range(1, len(pieces), 2)]
         for n, group in enumerate(groups):
             picked = look_up_dm(group, n)
-            (i, a), (j, d) = group[0][:2], (group[-1][0], group[-1][2])
-            add(nc.gpsimd, picked[:], i * E + a, j * E + d)
+            (i, a), (j, b) = group[0][:2], (group[-1][0], group[-1][2])
+            add(nc.gpsimd, picked[:], i * E + a, j * E + b)
             if a == PIECE:
-                store(i, 0 if i < last_block - 1 else PIECE, 3 * PIECE)
-            if a == 3 * PIECE:
+                store(i, 0 if i < last_block - 1 else PIECE, b)
+            if a > 2 * PIECE:
                 store(i, a, E)
                 if j == last_block - 1 > i:
                     store(j, 0, PIECE)
 
-        middle, late, start = LAST_VECTOR // 2, E - LAST_PIECE, last_block * E
-        by_vector = look_up_dm([(last_block, 0, LAST_VECTOR, True)], "v")
+        late = E - LAST_PIECE
+        nodes = LAST_VECTOR // K
+        by_vector = tile([P, K, nodes], F32, "picked_dmv")
+        window = dm[last_block][:].indirect(entries(src_list, 0, LAST_VECTOR))
+        nc.vector.tensor_copy(by_vector[:].rearrange("p j x -> p x j"), window)
         by_scalar = look_up_dm([(last_block, LAST_VECTOR, late, False)], "s")
         by_scalar_late = look_up_dm([(last_block, late, E, False)], "t")
-        for picked, a, b in (
-            (by_vector[:, :middle], 0, middle),
-            (by_vector[:, middle:], middle, LAST_VECTOR),
-            (by_scalar[:], LAST_VECTOR, late),
-            (by_scalar_late[:], late, E),
-        ):
-            add(nc.vector, picked, start + a, start + b)
+        for x in (0, nodes // 2):
+            run = slice(x, x + nodes // 2)
+            first = last_block * V + x
+            nc.vector.tensor_tensor(sums[:, first : first + nodes // 2], by_vector[:, 0, run], by_vector[:, 1, run], ALU.add)
+            store(last_block, K * x, K * x + nodes)
+        for picked, a, b in ((by_scalar[:], LAST_VECTOR, late), (by_scalar_late[:], late, E)):
+            add(nc.vector, picked, last_block * E + a, last_block * E + b)
             store(last_block, a, b)

from contextlib import ExitStack

import concourse.mybir as mybir

V, K, E, D, DV = 1024, 2, 2048, 512, 512
FLOPS = 2 * DV * D * E

F32 = mybir.dt.float32
BF16 = mybir.dt.bfloat16
I32 = mybir.dt.int32
U32 = mybir.dt.uint32
U16 = mybir.dt.uint16
U8 = mybir.dt.uint8
E4M3 = mybir.dt.float8_e4m3fn_x4
E5M2 = mybir.dt.float8_e5m2_x4
ALU = mybir.AluOpType
ACT = mybir.ActivationFunctionType

P = 128
PLANES = 4
PAIRS = PLANES // 2
CHUNK = 512
HALF = CHUNK // 2
CHUNKS = E // CHUNK
BLOCKS = D // P
PER_COLUMN = 16
RUN = 4
WINDOW = 4 * CHUNK

PIECE = E // 4
LONG_PIECE = PIECE + 128
LAST_VECTOR = 1024
LAST_PIECE = 384


def tile_attend_gmp_kernel(tc, dyT, hE, wm, offs, offs2, out):
    nc = tc.nc
    last_chunk, last_block = CHUNKS - 1, BLOCKS - 1
    with ExitStack() as ctx:
        keep = ctx.enter_context(tc.tile_pool(name="keep", bufs=1))
        psum = ctx.enter_context(tc.psum_pool(name="psum", bufs=1))

        def tile(shape, dtype, name):
            return keep.tile(shape, dtype, name=name, align_bytes=64)

        dst_list = keep.tile([P, E // PER_COLUMN], U16, name="dst_list")
        src_list = keep.tile([P, E // PER_COLUMN], U16, name="src_list")
        dy = [tile([P, WINDOW], F32, f"dy{t}") for t in range(PLANES)]
        h = {(c, u): tile([P, 2, CHUNK], F32, f"h{c}{u}") for c in range(CHUNKS) for u in range(PAIRS)}
        dz = [tile([P, CHUNK, PLANES], BF16, f"dz{c}") for c in range(CHUNKS)]
        dz_codes = [tile([P, CHUNK], U32, f"dz_codes{c}") for c in range(CHUNKS)]
        dz_scales = [tile([P, CHUNK], U8, f"dz_scales{c}") for c in range(CHUNKS)]
        dz_pairs = [tile([P, PAIRS, CHUNK, 2], BF16, f"pairs{c}") for c in range(CHUNKS)]
        w = tile([P, PLANES, D], F32, "w")
        w_bf16 = tile([P, D, PLANES], BF16, "w_bf16")
        w_scales = tile([P, D], U8, "w_scales")
        dm = [tile([P, E], F32, f"dm{i}") for i in range(BLOCKS)]
        sums = tile([P, BLOCKS * V], F32, "sums")
        dy_picked = {}

        dy_planes = dyT.rearrange("(p t) v -> p t v", t=PLANES)
        h_planes = hE.rearrange("(p t) e -> p t e", t=PLANES)
        w_planes = wm.rearrange("(p t) d -> p t d", t=PLANES)

        def edges(c, a=0, b=CHUNK):
            return slice(c * CHUNK + a, c * CHUNK + b)

        def entries(offsets, a, b):
            return offsets[:, a // PER_COLUMN : b // PER_COLUMN]

        def load_dy(t):
            nc.sync.dma_start(out=dy[t][:, :V], in_=dy_planes[:, t, :])

        def look_up_dy(c, buffer):
            for u in range(PAIRS):
                dy_picked[c, u] = tile([P, 2, CHUNK], F32, f"{buffer}{u}")
                for t in range(2):
                    window = dy[2 * u + t][:].indirect(entries(dst_list, c * CHUNK, (c + 1) * CHUNK))
                    if c == 0:
                        nc.vector.tensor_scalar(dy_picked[c, u][:, t, :], window, 2.0, 0.0, ALU.mult, ALU.add)
                    else:
                        nc.scalar.activation(dy_picked[c, u][:, t, :], window, ACT.Copy, scale=2.0)

        def make_pair(c, u, a=0, b=CHUNK):
            nc.vector.scalar_tensor_tensor(
                dz_pairs[c][:, u, a:b, :],
                h[c, u][:, :, a:b].rearrange("p t e -> p e t"),
                0.0,
                dy_picked[c, u][:, :, a:b].rearrange("p t e -> p e t"),
                ALU.max,
                ALU.mult,
            )

        def join_pairs(c, a=0, b=CHUNK):
            src = dz_pairs[c][:, :, a:b, :].rearrange("p u e t -> p u (e t)").bitcast(I32)
            dst = dz[c][:, a:b, :].rearrange("p e t -> p (e t)").bitcast(I32)
            nc.vector.tensor_copy(dst.rearrange("p (e u) -> p e u", u=PAIRS), src.rearrange("p u e -> p e u"))

        def quantize(codes, scales, values, fmt):
            nc.vector.quantize_mx(out=codes.bitcast(fmt), scales=scales, in_=values.rearrange("p c t -> p (c t)"))

        def quantize_dz(c, a=0, b=CHUNK):
            quantize(dz_codes[c][:, a:b], dz_scales[c][:, a:b], dz[c][:, a:b, :], E5M2)

        def make_dm(copy, bank, i, c, a=0, b=CHUNK):
            acc = psum.tile([P, b - a], F32, name=f"bank{bank}")
            nc.tensor.matmul_mx(
                out=acc[:],
                lhsT=w_codes[:, i * P : (i + 1) * P].bitcast(E4M3),
                lhsT_scale=w_scales[:, i * P : (i + 1) * P],
                rhs=dz_codes[c][:, a:b].bitcast(E5M2),
                rhs_scale=dz_scales[c][:, a:b],
                start=True,
                stop=True,
            )
            copy(dm[i][:, edges(c, a, b)], acc[:])

        def look_up_dm(pieces, name):
            picked = tile([P, sum(b - a for i, a, b, on_vector in pieces)], F32, f"picked_dm{name}")
            at = 0
            for i, a, b, on_vector in pieces:
                window = dm[i][:].indirect(entries(src_list, a, b))
                if on_vector:
                    nc.vector.tensor_copy(picked[:, at : at + b - a], window)
                else:
                    nc.scalar.activation(picked[:, at : at + b - a], window, ACT.Copy)
                at = at + b - a
            return picked

        def add(engine, picked, first, end):
            width = end - first
            engine.tensor_tensor(sums[:, first // K : end // K], picked[:, 0:width:K], picked[:, 1:width:K], ALU.add)

        def store(i, a, b):
            nc.sync.dma_start(out=out[i * P : (i + 1) * P, a // K : b // K], in_=sums[:, (i * E + a) // K : (i * E + b) // K])

        warm_in = tile([P, 1], F32, "warm_in")
        warm_out = tile([P, 1], F32, "warm_out")
        nc.gpsimd.memset(warm_in[:], 0.0)
        nc.scalar.activation(warm_out[:], warm_in[:], ACT.Copy)

        for t in range(PLANES):
            (nc.vector if t < PLANES // 2 else nc.gpsimd).memset(dy[t][:, V:], 0.0)

        load_dy(0)
        nc.sync.dma_start(dst_list[:], offs)
        for t in range(1, PLANES):
            load_dy(t)
        for c in range(CHUNKS):
            for u in range(PAIRS):
                nc.sync.dma_start(out=h[c, u][:], in_=h_planes[:, 2 * u : 2 * u + 2, edges(c)])
            if c == 1:
                nc.sync.dma_start(out=w[:], in_=w_planes)
        nc.sync.dma_start(src_list[:], offs2)

        for c in range(last_chunk):
            look_up_dy(c, f"picked_dy{c}")
        make_pair(0, 0)
        make_pair(0, 1)
        look_up_dy(last_chunk, "picked_dy0")

        make_pair(1, 0)
        join_pairs(0)
        make_pair(1, 1)
        quantize_dz(0)
        nc.vector.tensor_copy(
            w_bf16[:].rearrange("p (c i) t -> p c t i", i=RUN), w[:].rearrange("p t (c i) -> p c t i", i=RUN)
        )
        join_pairs(1)
        w_codes = tile([P, D], U32, "w_codes")
        quantize(w_codes[:], w_scales[:], w_bf16[:], E4M3)
        make_pair(2, 0)
        make_pair(2, 1)
        quantize_dz(1)
        join_pairs(2)
        make_pair(last_chunk, 0)
        quantize_dz(2)
        halves = ((0, HALF), (HALF, CHUNK))
        for a, b in halves:
            make_pair(last_chunk, 1, a, b)
        for a, b in halves:
            join_pairs(last_chunk, a, b)
        for a, b in halves:
            quantize_dz(last_chunk, a, b)

        for c in range(last_chunk):
            for i in range(BLOCKS):
                on_vector = (i, c) == (last_block, last_chunk - 1)
                make_dm(nc.vector.tensor_copy if on_vector else nc.scalar.copy, (c % 2) * BLOCKS + i, i, c)
        make_dm(nc.scalar.copy, BLOCKS, 0, last_chunk, 0, HALF)
        make_dm(nc.vector.tensor_copy, BLOCKS + 1, 0, last_chunk, HALF, CHUNK)
        for i in range(1, BLOCKS):
            make_dm(nc.scalar.copy, (BLOCKS + 1 + i) % (2 * BLOCKS), i, last_chunk)

        pieces = []
        for i in range(last_block):
            cuts = (0, PIECE, 2 * PIECE, 2 * PIECE + (PIECE if i < last_block - 1 else LONG_PIECE), E)
            pieces.extend((i, a, b, n % 2 == 0) for n, (a, b) in enumerate(zip(cuts, cuts[1:])))
        groups = [pieces[:1]] + [pieces[n : n + 2] for n in range(1, len(pieces), 2)]
        for n, group in enumerate(groups):
            picked = look_up_dm(group, n)
            (i, a), (j, b) = group[0][:2], (group[-1][0], group[-1][2])
            add(nc.gpsimd, picked[:], i * E + a, j * E + b)
            if a == PIECE:
                store(i, 0 if i < last_block - 1 else PIECE, b)
            if a > 2 * PIECE:
                store(i, a, E)
                if j == last_block - 1 > i:
                    store(j, 0, PIECE)

        late = E - LAST_PIECE
        nodes = LAST_VECTOR // K
        by_vector = tile([P, K, nodes], F32, "picked_dmv")
        window = dm[last_block][:].indirect(entries(src_list, 0, LAST_VECTOR))
        nc.vector.tensor_copy(by_vector[:].rearrange("p j x -> p x j"), window)
        by_scalar = look_up_dm([(last_block, LAST_VECTOR, late, False)], "s")
        by_scalar_late = look_up_dm([(last_block, late, E, False)], "t")
        for x in (0, nodes // 2):
            run = slice(x, x + nodes // 2)
            first = last_block * V + x
            nc.vector.tensor_tensor(sums[:, first : first + nodes // 2], by_vector[:, 0, run], by_vector[:, 1, run], ALU.add)
            store(last_block, K * x, K * x + nodes)
        for picked, a, b in ((by_scalar[:], LAST_VECTOR, late), (by_scalar_late[:], late, E)):
            add(nc.vector, picked, last_block * E + a, last_block * E + b)
            store(last_block, a, b)
